import numpy as np
import ml_dtypes


def mxq(x, axis, fmt="e4m3"):
    dtype, down = {"e4m3": (ml_dtypes.float8_e4m3fn, 7), "e5m2": (ml_dtypes.float8_e5m2, 14)}[fmt]
    v = np.moveaxis(np.asarray(x, np.float32).astype(ml_dtypes.bfloat16).astype(np.float64), axis, -1)
    blocks = v.reshape(v.shape[:-1] + (-1, 32))
    amax = np.abs(blocks).max(-1, keepdims=True)
    byte = np.maximum(np.where(amax > 0, np.frexp(amax)[1] - 1 + 127, 0) - down, 1)
    scale = np.exp2(byte - 127.0)
    codes = (blocks / scale).astype(np.float32).astype(dtype).astype(np.float64)
    return np.moveaxis((codes * scale).reshape(v.shape), -1, axis)


WIDE = False


def mx_kscale(k):
    if not WIDE:
        return np.ones(k)
    levels = np.array([10, -10, 5, -5, 0])
    if k % 512:
        return np.exp2(np.random.permutation(np.resize(levels, k // 32))).repeat(32)
    a = np.empty((k // 512, 16))
    for p in range(k // 512):
        a[p, :8] = np.random.permutation(np.resize(levels, 8))
        for g in range(8):
            far = levels[np.abs(levels - a[p, g]) >= 10]
            a[p, g + 8] = far[np.random.randint(len(far))]
    return np.exp2(a.ravel()).repeat(32)


BF16 = ml_dtypes.bfloat16


def bf(x):
    return np.asarray(x, np.float32).astype(BF16)


def f64(x):
    return np.asarray(x).astype(np.float64)


E2M1 = np.array([0.0, 0.5, 1.0, 1.5, 2.0, 3.0, 4.0, 6.0, -0.0, -0.5, -1.0, -1.5, -2.0, -3.0, -4.0, -6.0])


def pack_weight(w, fmt):
    k, n = w.shape
    w = f64(bf(w)).reshape(k // 32, 32, n)
    amax = np.abs(w).max(1)
    if fmt == "e4m3":
        byte = np.frexp(amax)[1] - 1 + 127 - 7
    else:
        mant, ex = np.frexp(amax / 6.0)
        byte = np.where(mant > 0.5, ex, ex - 1) + 127
    byte = np.clip(np.where(amax > 0, byte, 1), 1, 254)
    scaled = (w * np.exp2(127.0 - byte)[:, None, :]).reshape(k, n).astype(np.float32)
    by_word = np.ascontiguousarray(scaled.reshape(k // 512, 128, 4, n).transpose(0, 1, 3, 2))
    if fmt == "e4m3":
        words = by_word.astype(ml_dtypes.float8_e4m3fn).view(np.uint8)
    else:
        c = by_word.astype(ml_dtypes.float4_e2m1fn).view(np.uint8) & 0xF
        words = c[..., 0::2] | (c[..., 1::2] << 4)
    return np.ascontiguousarray(words), np.ascontiguousarray(byte.astype(np.uint8).reshape(k // 512, 16, n))


def unpack_weight(words, scales, fmt):
    g, p, n, _ = words.shape
    if fmt == "e4m3":
        vals = np.ascontiguousarray(words).view(ml_dtypes.float8_e4m3fn).astype(np.float64)
    else:
        nib = np.empty((g, p, n, 4), np.uint8)
        nib[..., 0::2] = words & 0xF
        nib[..., 1::2] = words >> 4
        vals = E2M1[nib]
    vals = vals * np.repeat(np.exp2(scales.astype(np.float64) - 127.0), 8, axis=1)[..., None]
    return vals.transpose(0, 1, 3, 2).reshape(g * 512, n)
def pack4(w):
    words, scales = pack_weight(w, "e2m1")
    return words.reshape(words.shape[0], 128, -1), scales


def unpack4(words, scales):
    return unpack_weight(words.reshape(words.shape[0], 128, -1, 2), scales, "e2m1")


G, P, K, N, D = 8, 512, 1024, 512, 512


def draw0():
    s = mx_kscale(K)
    t = mx_kscale(N)
    coef = np.random.standard_normal((G, K, N)) / np.sqrt(K) / s[:, None]
    bank = np.random.standard_normal((G, N, 2 * D)) / np.sqrt(N) / t[:, None]
    coef_words, coef_scales = pack4(coef.reshape(G * K, N))
    bank_words, bank_scales = pack4(bank.reshape(G * N, 2 * D))
    return {"past": bf(np.random.standard_normal((G, P, K)) * s),
            "now": bf(np.random.standard_normal((G, P, N))),
            "taper": bf((1 + 0.1 * np.random.standard_normal((G, N))) * t),
            "coef_words": coef_words, "coef_scales": coef_scales,
            "bank_words": bank_words, "bank_scales": bank_scales}


def core(past, now, taper, coef_words, coef_scales, bank_words, bank_scales):
    coef = unpack4(coef_words, coef_scales).reshape(G, K, N)
    bank = unpack4(bank_words, bank_scales).reshape(G, N, 2 * D)
    pred = mxq(f64(past), 2, "e4m3") @ coef
    e = (f64(now) - pred) * f64(taper)[:, None, :]
    y = mxq(e, 2, "e4m3") @ bank
    return np.sqrt(np.square(y[:, :, :D]) + np.square(y[:, :, D:]))


def e4m3fn_bytes(y):
    return np.clip(np.asarray(y, np.float64), -448.0, 448.0).astype(np.float32).astype(ml_dtypes.float8_e4m3fn).view(np.uint8)


def e4m3fn_values(b):
    return np.asarray(b, np.uint8).view(ml_dtypes.float8_e4m3fn).astype(np.float64)


def setup_inputs():
    d = draw0()
    x0 = np.asarray(d['past']).astype(np.float64)
    s = (np.max(np.abs(x0), axis=(0, 1), keepdims=True) / 448.0).astype(np.float32)
    out = {}
    for k, v in d.items():
        if k == 'past':
            out['past_bytes'] = e4m3fn_bytes(x0 / s.astype(np.float64))
            out['past_scale'] = s
        else:
            out[k] = v
    return out


def reference(past_bytes, past_scale, now, taper, coef_words, coef_scales, bank_words, bank_scales):
    return core(e4m3fn_values(past_bytes) * past_scale.astype(np.float64), now, taper, coef_words, coef_scales, bank_words, bank_scales)

@@ -1,0 +1,286 @@
+from contextlib import ExitStack
+
+import concourse.mybir as mybir
+from concourse.masks import make_identity
+
+BEAMS, PINGS, PAST, NOW, DOPPLER = 8, 512, 1024, 512, 512
+FLOPS = 2 * BEAMS * PINGS * (PAST * NOW + NOW * 2 * DOPPLER)
+
+P = 128
+UNITS = PINGS // P
+STEPS = BEAMS * UNITS
+GROUPS = PAST // 512
+
+F32 = mybir.dt.float32
+BF16 = mybir.dt.bfloat16
+U32 = mybir.dt.uint32
+I32 = mybir.dt.int32
+U8 = mybir.dt.uint8
+FP8 = mybir.dt.float8_e4m3fn
+FP8X4 = mybir.dt.float8_e4m3fn_x4
+FP4X4 = mybir.dt.float4_e2m1fn_x4
+ALU = mybir.AluOpType
+ACT = mybir.ActivationFunctionType
+
+
+def tile_reverb_prewhiten_replicas_s14_kernel(
+    tc, past_bytes, past_scale, now, taper, coef_words, coef_scales, bank_words, bank_scales, out
+):
+    nc = tc.nc
+    with ExitStack() as ctx:
+        keep = ctx.enter_context(tc.tile_pool(name="keep", bufs=1))
+        inp = ctx.enter_context(tc.tile_pool(name="inp", bufs=6))
+        work = ctx.enter_context(tc.tile_pool(name="work", bufs=3))
+        outs = ctx.enter_context(tc.tile_pool(name="outs", bufs=STEPS))
+        psum2 = ctx.enter_context(tc.psum_pool(name="psum2", bufs=2))
+        psum1 = ctx.enter_context(tc.psum_pool(name="psum1", bufs=1))
+
+        beams = {}
+        on_vector = range(STEPS - 4, STEPS)
+
+        def load_past(b, split):
+            past_u8 = inp.tile([P, UNITS, PAST], U8, align_bytes=64)
+            src = past_bytes[b].rearrange("(r j) k -> r j k", j=UNITS)
+            if split:
+                for j in range(UNITS):
+                    nc.sync.dma_start(out=past_u8[:, j, :], in_=src[:, j, :])
+            else:
+                nc.sync.dma_start(out=past_u8[:], in_=src)
+            return past_u8
+
+        def load_now(b):
+            now_sb = inp.tile([P, UNITS, NOW], BF16, align_bytes=64)
+            nc.sync.dma_start(out=now_sb[:], in_=now[b].rearrange("(r j) n -> r j n", j=UNITS))
+            return now_sb
+
+        def load_coef(b):
+            coef = inp.tile([P, GROUPS, 2 * NOW], U8, align_bytes=64)
+            nc.sync.dma_start(
+                out=coef[:].bitcast(I32),
+                in_=coef_words[GROUPS * b : GROUPS * (b + 1)].rearrange("g p n -> p g n").bitcast(I32),
+            )
+            return coef
+
+        def load_bank(b):
+            bank = inp.tile([P, 4 * DOPPLER], U8, align_bytes=64)
+            nc.sync.dma_start(out=bank[:].bitcast(I32), in_=bank_words[b].bitcast(I32))
+            return bank
+
+        coef_s = keep.tile([P, BEAMS * GROUPS, NOW], U8, align_bytes=64)
+        bank_s = keep.tile([P, BEAMS, 2 * DOPPLER], U8, align_bytes=64)
+        scale_sb = keep.tile([P, PAST], F32, align_bytes=64)
+        taper_sb = keep.tile([P, BEAMS, 4], BF16, align_bytes=64)
+        ident = keep.tile([P, P], F32, align_bytes=64)
+        warm = keep.tile([P, 1], F32)
+
+        ident16 = keep.tile([P, P], BF16, align_bytes=64)
+        taper_x = keep.tile([P, BEAMS, P, 4], BF16, align_bytes=64)
+
+        nc.sync.dma_start(out=scale_sb[:], in_=past_scale.rearrange("a b k -> (a b k)").partition_broadcast(P))
+        past0 = load_past(0, True)
+        nc.vector.memset(warm[:], 1.0)
+        nc.vector.memset(coef_s[:].rearrange("p a n -> p (a n)").bitcast(I32), 0)
+        make_identity(nc, ident[:])
+        nc.gpsimd.memset(bank_s[:].rearrange("p a n -> p (a n)").bitcast(I32), 0)
+        nc.scalar.activation(out=warm[:], in_=warm[:], func=ACT.Sqrt)
+        nc.scalar.copy(out=ident16[:], in_=ident[:])
+        for q in range(4):
+            nc.sync.dma_start(
+                out=coef_s[32 * q : 32 * q + 4, :, :].bitcast(I32),
+                in_=coef_scales[:, 4 * q : 4 * q + 4, :].rearrange("a r n -> r a n").bitcast(I32),
+            )
+        coef0 = load_coef(0)
+        now0 = load_now(0)
+        nc.sync.dma_start(out=taper_sb[:], in_=taper.rearrange("b (p t) -> p b t", t=4))
+        for q in range(4):
+            nc.sync.dma_start(
+                out=bank_s[32 * q : 32 * q + 4, :, :].bitcast(I32),
+                in_=bank_scales[:, 4 * q : 4 * q + 4, :].rearrange("a r n -> r a n").bitcast(I32),
+            )
+        bank0 = load_bank(0)
+        beams[0] = (past0, now0, coef0, bank0)
+
+        def load_beam(b):
+            past_n = load_past(b, False)
+            coef_n = load_coef(b)
+            now_n = load_now(b)
+            bank_n = load_bank(b)
+            beams[b] = (past_n, now_n, coef_n, bank_n)
+
+        load_beam(1)
+        load_beam(2)
+
+        past16s, tps, groupeds, codes_p, preds, ds, dts, e16s, codes_e, ys, sqs, sums = (
+            {}, {}, {}, {}, {}, {}, {}, {}, {}, {}, {}, {}
+        )
+
+        def spread_taper(b):
+            nc.scalar.copy(
+                out=taper_x[:, b : b + 2, :, :].bitcast(F32),
+                in_=taper_sb[:, b : b + 2, :].bitcast(F32).unsqueeze(2).to_broadcast([P, 2, P, 2]),
+            )
+
+        def widen(i):
+            past_u8 = beams[i // UNITS][0]
+            past16 = work.tile([P, PAST], BF16, align_bytes=64)
+            nc.vector.tensor_tensor(
+                out=past16[:], in0=past_u8[:, i % UNITS, :].bitcast(FP8), in1=scale_sb[:], op=ALU.mult
+            )
+            past16s[i] = past16
+
+        def turn_past(i):
+            tp = psum2.tile([P, 512], F32)
+            words = past16s.pop(i)[:].bitcast(F32)
+            for u in range(2):
+                for g in range(GROUPS):
+                    col = u * 256 + g * P
+                    nc.tensor.transpose(
+                        tp[:, col : col + P], words[:, 256 * g + u : 256 * (g + 1) : 2], ident[:]
+                    )
+            tps[i] = tp
+
+        def scale_past(i):
+            grouped = work.tile([P, GROUPS, P, 4], BF16, align_bytes=64)
+            nc.scalar.copy(
+                out=grouped[:].rearrange("p g r t -> p (g r t)").bitcast(F32).rearrange("p (q u) -> p q u", u=2),
+                in_=tps.pop(i)[:].rearrange("p (u q) -> p q u", u=2),
+            )
+            groupeds[i] = grouped
+
+        def quant_past(i):
+            pc = work.tile([P, GROUPS, P], U32, align_bytes=64)
+            ps = work.tile([P, GROUPS, P], U8, align_bytes=64)
+            nc.vector.quantize_mx(
+                out=pc[:].rearrange("p g r -> p (g r)").bitcast(FP8X4),
+                scales=ps[:].rearrange("p g r -> p (g r)"),
+                in_=groupeds.pop(i)[:].rearrange("p g r t -> p (g r t)"),
+            )
+            codes_p[i] = (pc, ps)
+
+        def predict(i):
+            b = i // UNITS
+            coef = beams[b][2]
+            pc, ps = codes_p.pop(i)
+            pred = psum2.tile([P, NOW], F32)
+            for g in range(GROUPS):
+                nc.tensor.matmul_mx(
+                    out=pred[:],
+                    lhsT=pc[:, g, :].bitcast(FP8X4),
+                    lhsT_scale=ps[:, g, :],
+                    rhs=coef[:, g, :].bitcast(FP4X4),
+                    rhs_scale=coef_s[:, GROUPS * b + g, :],
+                    start=(g == 0),
+                    stop=(g == GROUPS - 1),
+                )
+            preds[i] = pred
+
+        def subtract(i):
+            d = work.tile([P, 4, P], F32, align_bytes=64)
+            pred = preds.pop(i)[:].rearrange("r (p t) -> r t p", t=4)
+            if i in on_vector:
+                nc.vector.tensor_tensor(
+                    out=d[:], in0=beams[i // UNITS][1][:, i % UNITS, :].rearrange("r (p t) -> r t p", t=4), in1=pred,
+                    op=ALU.subtract,
+                )
+            else:
+                nc.scalar.activation(out=d[:], in_=pred, func=ACT.Copy, scale=-1.0)
+            ds[i] = d
+
+        def turn_d(i):
+            dt = psum2.tile([P, 4, P], F32)
+            d = ds.pop(i)
+            now_u = beams[i // UNITS][1][:, i % UNITS, :]
+            if i in on_vector:
+                for t in range(4):
+                    nc.tensor.transpose(dt[:, t, :], d[:, t, :], ident[:])
+            else:
+                for t in range(4):
+                    nc.tensor.matmul(dt[:, t, :], lhsT=now_u[:, t::4], rhs=ident16[:], start=(t == 0), stop=False)
+                for t in range(4):
+                    nc.tensor.matmul(
+                        dt[:, t, :], lhsT=d[:, t, :], rhs=ident[:], is_transpose=True, start=False, stop=(t == 3)
+                    )
+            dts[i] = dt
+
+        def apply_taper(i):
+            e16 = work.tile([P, P, 4], BF16, align_bytes=64)
+            nc.vector.tensor_tensor(
+                out=e16[:],
+                in0=dts.pop(i)[:].rearrange("p t r -> p r t"),
+                in1=taper_x[:, i // UNITS, :, :],
+                op=ALU.mult,
+            )
+            e16s[i] = e16
+
+        def quant_e(i):
+            ec = work.tile([P, P], U32, align_bytes=64)
+            es = work.tile([P, P], U8, align_bytes=64)
+            nc.vector.quantize_mx(
+                out=ec[:].bitcast(FP8X4), scales=es[:], in_=e16s.pop(i)[:].rearrange("p r t -> p (r t)")
+            )
+            codes_e[i] = (ec, es)
+
+        def correlate(i):
+            b = i // UNITS
+            bank = beams[b][3]
+            ec, es = codes_e.pop(i)
+            y_i = psum1.tile([P, DOPPLER], F32)
+            y_q = psum1.tile([P, DOPPLER], F32)
+            for h, y in enumerate((y_i, y_q)):
+                nc.tensor.matmul_mx(
+                    out=y[:],
+                    lhsT=ec[:].bitcast(FP8X4),
+                    lhsT_scale=es[:],
+                    rhs=bank[:, 2 * DOPPLER * h : 2 * DOPPLER * (h + 1)].bitcast(FP4X4),
+                    rhs_scale=bank_s[:, b, DOPPLER * h : DOPPLER * (h + 1)],
+                    start=True,
+                    stop=True,
+                )
+            ys[i] = (y_i, y_q)
+
+        def square_i(i):
+            sq = work.tile([P, 2, DOPPLER], F32, align_bytes=64)
+            nc.scalar.activation(out=sq[:, 0, :], in_=ys[i][0][:], func=ACT.Square)
+            sqs[i] = sq
+
+        def square_q(i):
+            nc.scalar.activation(out=sqs[i][:, 1, :], in_=ys.pop(i)[1][:], func=ACT.Square)
+
+        def add(i):
+            power = work.tile([P, DOPPLER], F32, align_bytes=64)
+            sq = sqs.pop(i)
+            nc.vector.tensor_tensor(out=power[:], in0=sq[:, 0, :], in1=sq[:, 1, :], op=ALU.add)
+            sums[i] = power
+
+        def root(i):
+            env = outs.tile([P, DOPPLER], F32, align_bytes=64)
+            nc.scalar.activation(out=env[:], in_=sums.pop(i)[:], func=ACT.Sqrt)
+            nc.sync.dma_start(
+                out=out[i // UNITS].rearrange("(r j) d -> r j d", j=UNITS)[:, i % UNITS, :], in_=env[:]
+            )
+
+        with tc.manual_schedule():
+            for s in range(STEPS + 9):
+                plan = (
+                    (widen, s),
+                    (subtract, s - 4),
+                    (predict, s - 3),
+                    (apply_taper, s - 5),
+                    (root, s - 9),
+                    (correlate, s - 6),
+                    (add, s - 8),
+                    (scale_past, s - 1),
+                    (turn_d, s - 4),
+                    (quant_e, s - 5),
+                    (quant_past, s - 2),
+                    (square_i, s - 6),
+                    (square_q, s - 6),
+                    (turn_past, s),
+                )
+                if s % UNITS == 0 and s // UNITS + 3 < BEAMS:
+                    load_beam(s // UNITS + 3)
+                for stage, i in plan:
+                    if 0 <= i < STEPS:
+                        stage(i)
+                if 3 <= s < 3 + BEAMS // 2:
+                    spread_taper(2 * (s - 3))

@@ -10,6 +10,9 @@ P = 128
 UNITS = PINGS // P
 STEPS = BEAMS * UNITS
 GROUPS = PAST // 512
+AHEAD = 2
+ADD_LAG = 4
+TAIL = 3
 
 F32 = mybir.dt.float32
 BF16 = mybir.dt.bfloat16
@@ -29,146 +32,127 @@ def tile_reverb_prewhiten_replicas_s14_kernel(
     nc = tc.nc
     with ExitStack() as ctx:
         keep = ctx.enter_context(tc.tile_pool(name="keep", bufs=1))
-        inp = ctx.enter_context(tc.tile_pool(name="inp", bufs=6))
-        work = ctx.enter_context(tc.tile_pool(name="work", bufs=3))
-        outs = ctx.enter_context(tc.tile_pool(name="outs", bufs=STEPS))
+        inp = ctx.enter_context(tc.tile_pool(name="inp", bufs=AHEAD + 2))
+        work = ctx.enter_context(tc.tile_pool(name="work", bufs=4))
+        outs = ctx.enter_context(tc.tile_pool(name="outs", bufs=16))
         psum2 = ctx.enter_context(tc.psum_pool(name="psum2", bufs=2))
         psum1 = ctx.enter_context(tc.psum_pool(name="psum1", bufs=1))
+        ctx.enter_context(tc.manual_schedule())
 
-        beams = {}
-        on_vector = range(STEPS - 4, STEPS)
+        coef_s = [keep.tile([P, GROUPS * NOW], U8, align_bytes=64, name="coef_s%d" % b) for b in range(BEAMS)]
+        bank_s = [keep.tile([P, 2 * DOPPLER], U8, align_bytes=64, name="bank_s%d" % b) for b in range(BEAMS)]
+        scale_sb = keep.tile([P, GROUPS, 4], F32, align_bytes=64)
+        scale_x = keep.tile([P, GROUPS, P, 4], F32, align_bytes=64)
+        taper_sb = keep.tile([P, BEAMS, 4], BF16, align_bytes=64)
+        taper_x = keep.tile([P, BEAMS, P, 4], BF16, align_bytes=64)
+        ident = keep.tile([P, P], F32, align_bytes=64)
+        ident16 = keep.tile([P, P], BF16, align_bytes=64)
 
-        def load_past(b, split):
+        pasts, nows, coefs, banks = {}, {}, {}, {}
+
+        def load_past(b, pieces):
             past_u8 = inp.tile([P, UNITS, PAST], U8, align_bytes=64)
             src = past_bytes[b].rearrange("(r j) k -> r j k", j=UNITS)
-            if split:
-                for j in range(UNITS):
-                    nc.sync.dma_start(out=past_u8[:, j, :], in_=src[:, j, :])
-            else:
-                nc.sync.dma_start(out=past_u8[:], in_=src)
-            return past_u8
+            for piece in pieces:
+                nc.sync.dma_start(out=past_u8[:, piece, :], in_=src[:, piece, :])
+            pasts[b] = past_u8
 
         def load_now(b):
             now_sb = inp.tile([P, UNITS, NOW], BF16, align_bytes=64)
             nc.sync.dma_start(out=now_sb[:], in_=now[b].rearrange("(r j) n -> r j n", j=UNITS))
-            return now_sb
+            nows[b] = now_sb
 
         def load_coef(b):
             coef = inp.tile([P, GROUPS, 2 * NOW], U8, align_bytes=64)
-            nc.sync.dma_start(
-                out=coef[:].bitcast(I32),
-                in_=coef_words[GROUPS * b : GROUPS * (b + 1)].rearrange("g p n -> p g n").bitcast(I32),
-            )
-            return coef
+            groups = slice(GROUPS * b, GROUPS * (b + 1))
+            nc.sync.dma_start(out=coef[:].bitcast(I32), in_=coef_words[groups].rearrange("g p n -> p g n").bitcast(I32))
+            for r in range(4):
+                nc.sync.dma_start(
+                    out=coef_s[b][r:P:32, :].rearrange("q (g n) -> q g n", g=GROUPS).bitcast(I32),
+                    in_=coef_scales[groups, r:16:4, :].rearrange("g q n -> q g n").bitcast(I32),
+                )
+            coefs[b] = coef
 
         def load_bank(b):
             bank = inp.tile([P, 4 * DOPPLER], U8, align_bytes=64)
             nc.sync.dma_start(out=bank[:].bitcast(I32), in_=bank_words[b].bitcast(I32))
-            return bank
-
-        coef_s = keep.tile([P, BEAMS * GROUPS, NOW], U8, align_bytes=64)
-        bank_s = keep.tile([P, BEAMS, 2 * DOPPLER], U8, align_bytes=64)
-        scale_sb = keep.tile([P, PAST], F32, align_bytes=64)
-        taper_sb = keep.tile([P, BEAMS, 4], BF16, align_bytes=64)
-        ident = keep.tile([P, P], F32, align_bytes=64)
-        warm = keep.tile([P, 1], F32)
-
-        ident16 = keep.tile([P, P], BF16, align_bytes=64)
-        taper_x = keep.tile([P, BEAMS, P, 4], BF16, align_bytes=64)
-
-        nc.sync.dma_start(out=scale_sb[:], in_=past_scale.rearrange("a b k -> (a b k)").partition_broadcast(P))
-        past0 = load_past(0, True)
-        nc.vector.memset(warm[:], 1.0)
-        nc.vector.memset(coef_s[:].rearrange("p a n -> p (a n)").bitcast(I32), 0)
-        make_identity(nc, ident[:])
-        nc.gpsimd.memset(bank_s[:].rearrange("p a n -> p (a n)").bitcast(I32), 0)
-        nc.scalar.activation(out=warm[:], in_=warm[:], func=ACT.Sqrt)
-        nc.scalar.copy(out=ident16[:], in_=ident[:])
-        for q in range(4):
-            nc.sync.dma_start(
-                out=coef_s[32 * q : 32 * q + 4, :, :].bitcast(I32),
-                in_=coef_scales[:, 4 * q : 4 * q + 4, :].rearrange("a r n -> r a n").bitcast(I32),
-            )
-        coef0 = load_coef(0)
-        now0 = load_now(0)
-        nc.sync.dma_start(out=taper_sb[:], in_=taper.rearrange("b (p t) -> p b t", t=4))
-        for q in range(4):
-            nc.sync.dma_start(
-                out=bank_s[32 * q : 32 * q + 4, :, :].bitcast(I32),
-                in_=bank_scales[:, 4 * q : 4 * q + 4, :].rearrange("a r n -> r a n").bitcast(I32),
-            )
-        bank0 = load_bank(0)
-        beams[0] = (past0, now0, coef0, bank0)
+            for r in range(4):
+                nc.sync.dma_start(out=bank_s[b][r:P:32, :].bitcast(I32), in_=bank_scales[b, r:16:4, :].bitcast(I32))
+            banks[b] = bank
 
         def load_beam(b):
-            past_n = load_past(b, False)
-            coef_n = load_coef(b)
-            now_n = load_now(b)
-            bank_n = load_bank(b)
-            beams[b] = (past_n, now_n, coef_n, bank_n)
+            load_past(b, [slice(0, UNITS)])
+            load_coef(b)
+            load_now(b)
+            load_bank(b)
 
-        load_beam(1)
-        load_beam(2)
+        make_identity(nc, ident[:])
+        for b in range(BEAMS):
+            nc.vector.memset(coef_s[b][:].bitcast(I32), 0)
+            nc.vector.memset(bank_s[b][:].bitcast(I32), 0)
+        nc.scalar.activation(out=ident16[:], in_=ident[:], func=ACT.Sqrt)
 
-        past16s, tps, groupeds, codes_p, preds, ds, dts, e16s, codes_e, ys, sqs, sums = (
-            {}, {}, {}, {}, {}, {}, {}, {}, {}, {}, {}, {}
-        )
+        nc.sync.dma_start(out=scale_sb[:], in_=past_scale.rearrange("a b (g p t) -> p (a b g) t", p=P, t=4))
+        load_past(0, [slice(0, 1), slice(1, UNITS)])
+        load_coef(0)
+        nc.sync.dma_start(out=taper_sb[:], in_=taper.rearrange("b (p t) -> p b t", t=4))
+        load_now(0)
+        load_bank(0)
+        for b in range(1, AHEAD):
+            load_beam(b)
 
-        def spread_taper(b):
-            nc.scalar.copy(
-                out=taper_x[:, b : b + 2, :, :].bitcast(F32),
-                in_=taper_sb[:, b : b + 2, :].bitcast(F32).unsqueeze(2).to_broadcast([P, 2, P, 2]),
+        nc.vector.tensor_copy(out=scale_x[:], in_=scale_sb[:].unsqueeze(2).to_broadcast([P, GROUPS, P, 4]))
+
+        def spread_taper():
+            nc.vector.tensor_copy(
+                out=taper_x[:].bitcast(F32), in_=taper_sb[:].bitcast(F32).unsqueeze(2).to_broadcast([P, BEAMS, P, 2])
             )
+
+        raws, turned, groupeds, codes_p, preds, ds, dts, e16s, codes_e, ys, sqs, sums = ({} for k in range(12))
+
+        def vector_subtracts(i):
+            return i % 2 == 1 or i >= STEPS - TAIL
 
         def widen(i):
-            past_u8 = beams[i // UNITS][0]
-            past16 = work.tile([P, PAST], BF16, align_bytes=64)
-            nc.vector.tensor_tensor(
-                out=past16[:], in0=past_u8[:, i % UNITS, :].bitcast(FP8), in1=scale_sb[:], op=ALU.mult
-            )
-            past16s[i] = past16
+            raw = work.tile([P, PAST], BF16, align_bytes=64)
+            nc.scalar.copy(out=raw[:], in_=pasts[i // UNITS][:, i % UNITS, :].bitcast(FP8))
+            raws[i] = raw
 
         def turn_past(i):
-            tp = psum2.tile([P, 512], F32)
-            words = past16s.pop(i)[:].bitcast(F32)
-            for u in range(2):
-                for g in range(GROUPS):
-                    col = u * 256 + g * P
-                    nc.tensor.transpose(
-                        tp[:, col : col + P], words[:, 256 * g + u : 256 * (g + 1) : 2], ident[:]
-                    )
-            tps[i] = tp
+            tp = psum2.tile([P, 2, GROUPS * P], F32)
+            words = raws.pop(i)[:].bitcast(F32)
+            for g in range(GROUPS):
+                for u in range(2):
+                    nc.tensor.transpose(tp[:, u, P * g : P * (g + 1)], words[:, 256 * g + u : 256 * (g + 1) : 2], ident[:])
+            turned[i] = tp
 
         def scale_past(i):
-            grouped = work.tile([P, GROUPS, P, 4], BF16, align_bytes=64)
-            nc.scalar.copy(
-                out=grouped[:].rearrange("p g r t -> p (g r t)").bitcast(F32).rearrange("p (q u) -> p q u", u=2),
-                in_=tps.pop(i)[:].rearrange("p (u q) -> p q u", u=2),
+            grouped = work.tile([P, PAST], BF16, align_bytes=64, bufs=6)
+            nc.vector.tensor_tensor(
+                out=grouped[:].rearrange("p (q u e) -> p q u e", u=2, e=2),
+                in0=scale_x[:].rearrange("p g r (u e) -> p (g r) u e", u=2),
+                in1=turned.pop(i)[:].bitcast(BF16).rearrange("p u (q e) -> p q u e", e=2),
+                op=ALU.mult,
             )
             groupeds[i] = grouped
 
         def quant_past(i):
-            pc = work.tile([P, GROUPS, P], U32, align_bytes=64)
-            ps = work.tile([P, GROUPS, P], U8, align_bytes=64)
-            nc.vector.quantize_mx(
-                out=pc[:].rearrange("p g r -> p (g r)").bitcast(FP8X4),
-                scales=ps[:].rearrange("p g r -> p (g r)"),
-                in_=groupeds.pop(i)[:].rearrange("p g r t -> p (g r t)"),
-            )
+            pc = work.tile([P, GROUPS * P], U32, align_bytes=64)
+            ps = work.tile([P, GROUPS * P], U8, align_bytes=64)
+            nc.vector.quantize_mx(out=pc[:].bitcast(FP8X4), scales=ps[:], in_=groupeds[i][:])
             codes_p[i] = (pc, ps)
 
         def predict(i):
             b = i // UNITS
-            coef = beams[b][2]
             pc, ps = codes_p.pop(i)
             pred = psum2.tile([P, NOW], F32)
             for g in range(GROUPS):
                 nc.tensor.matmul_mx(
                     out=pred[:],
-                    lhsT=pc[:, g, :].bitcast(FP8X4),
-                    lhsT_scale=ps[:, g, :],
-                    rhs=coef[:, g, :].bitcast(FP4X4),
-                    rhs_scale=coef_s[:, GROUPS * b + g, :],
+                    lhsT=pc[:, P * g : P * (g + 1)].bitcast(FP8X4),
+                    lhsT_scale=ps[:, P * g : P * (g + 1)],
+                    rhs=coefs[b][:, g, :].bitcast(FP4X4),
+                    rhs_scale=coef_s[b][:, NOW * g : NOW * (g + 1)],
                     start=(g == 0),
                     stop=(g == GROUPS - 1),
                 )
@@ -177,9 +161,9 @@ def tile_reverb_prewhiten_replicas_s14_kernel(
         def subtract(i):
             d = work.tile([P, 4, P], F32, align_bytes=64)
             pred = preds.pop(i)[:].rearrange("r (p t) -> r t p", t=4)
-            if i in on_vector:
+            if vector_subtracts(i):
                 nc.vector.tensor_tensor(
-                    out=d[:], in0=beams[i // UNITS][1][:, i % UNITS, :].rearrange("r (p t) -> r t p", t=4), in1=pred,
+                    out=d[:], in0=nows[i // UNITS][:, i % UNITS, :].rearrange("r (p t) -> r t p", t=4), in1=pred,
                     op=ALU.subtract,
                 )
             else:
@@ -189,8 +173,8 @@ def tile_reverb_prewhiten_replicas_s14_kernel(
         def turn_d(i):
             dt = psum2.tile([P, 4, P], F32)
             d = ds.pop(i)
-            now_u = beams[i // UNITS][1][:, i % UNITS, :]
-            if i in on_vector:
+            now_u = nows[i // UNITS][:, i % UNITS, :]
+            if vector_subtracts(i):
                 for t in range(4):
                     nc.tensor.transpose(dt[:, t, :], d[:, t, :], ident[:])
             else:
@@ -206,8 +190,8 @@ def tile_reverb_prewhiten_replicas_s14_kernel(
             e16 = work.tile([P, P, 4], BF16, align_bytes=64)
             nc.vector.tensor_tensor(
                 out=e16[:],
-                in0=dts.pop(i)[:].rearrange("p t r -> p r t"),
-                in1=taper_x[:, i // UNITS, :, :],
+                in0=taper_x[:, i // UNITS, :, :],
+                in1=dts.pop(i)[:].rearrange("p t r -> p r t"),
                 op=ALU.mult,
             )
             e16s[i] = e16
@@ -222,7 +206,6 @@ def tile_reverb_prewhiten_replicas_s14_kernel(
 
         def correlate(i):
             b = i // UNITS
-            bank = beams[b][3]
             ec, es = codes_e.pop(i)
             y_i = psum1.tile([P, DOPPLER], F32)
             y_q = psum1.tile([P, DOPPLER], F32)
@@ -231,56 +214,57 @@ def tile_reverb_prewhiten_replicas_s14_kernel(
                     out=y[:],
                     lhsT=ec[:].bitcast(FP8X4),
                     lhsT_scale=es[:],
-                    rhs=bank[:, 2 * DOPPLER * h : 2 * DOPPLER * (h + 1)].bitcast(FP4X4),
-                    rhs_scale=bank_s[:, b, DOPPLER * h : DOPPLER * (h + 1)],
+                    rhs=banks[b][:, 2 * DOPPLER * h : 2 * DOPPLER * (h + 1)].bitcast(FP4X4),
+                    rhs_scale=bank_s[b][:, DOPPLER * h : DOPPLER * (h + 1)],
                     start=True,
                     stop=True,
                 )
             ys[i] = (y_i, y_q)
 
-        def square_i(i):
+        def square(i):
             sq = work.tile([P, 2, DOPPLER], F32, align_bytes=64)
-            nc.scalar.activation(out=sq[:, 0, :], in_=ys[i][0][:], func=ACT.Square)
+            for h, y in enumerate(ys.pop(i)):
+                nc.scalar.activation(out=sq[:, h, :], in_=y[:], func=ACT.Square)
             sqs[i] = sq
 
-        def square_q(i):
-            nc.scalar.activation(out=sqs[i][:, 1, :], in_=ys.pop(i)[1][:], func=ACT.Square)
-
         def add(i):
-            power = work.tile([P, DOPPLER], F32, align_bytes=64)
             sq = sqs.pop(i)
-            nc.vector.tensor_tensor(out=power[:], in0=sq[:, 0, :], in1=sq[:, 1, :], op=ALU.add)
+            if i + ADD_LAG < STEPS:
+                power = groupeds.pop(i + ADD_LAG)[:].bitcast(F32)
+                nc.gpsimd.tensor_tensor(out=power, in0=sq[:, 0, :], in1=sq[:, 1, :], op=ALU.add)
+            else:
+                total = work.tile([P, DOPPLER], F32, align_bytes=64)
+                power = total[:]
+                nc.vector.tensor_tensor(out=power, in0=sq[:, 0, :], in1=sq[:, 1, :], op=ALU.add)
             sums[i] = power
 
         def root(i):
             env = outs.tile([P, DOPPLER], F32, align_bytes=64)
-            nc.scalar.activation(out=env[:], in_=sums.pop(i)[:], func=ACT.Sqrt)
+            nc.scalar.activation(out=env[:], in_=sums.pop(i), func=ACT.Sqrt)
             nc.sync.dma_start(
                 out=out[i // UNITS].rearrange("(r j) d -> r j d", j=UNITS)[:, i % UNITS, :], in_=env[:]
             )
 
-        with tc.manual_schedule():
-            for s in range(STEPS + 9):
-                plan = (
-                    (widen, s),
-                    (subtract, s - 4),
-                    (predict, s - 3),
-                    (apply_taper, s - 5),
-                    (root, s - 9),
-                    (correlate, s - 6),
-                    (add, s - 8),
-                    (scale_past, s - 1),
-                    (turn_d, s - 4),
-                    (quant_e, s - 5),
-                    (quant_past, s - 2),
-                    (square_i, s - 6),
-                    (square_q, s - 6),
-                    (turn_past, s),
-                )
-                if s % UNITS == 0 and s // UNITS + 3 < BEAMS:
-                    load_beam(s // UNITS + 3)
-                for stage, i in plan:
-                    if 0 <= i < STEPS:
-                        stage(i)
-                if 3 <= s < 3 + BEAMS // 2:
-                    spread_taper(2 * (s - 3))
+        for s in range(-2, STEPS + 7):
+            plan = (
+                (correlate, s - 4),
+                (predict, s - 1),
+                (turn_d, s - 2),
+                (turn_past, s + 1),
+                (root, s - 6),
+                (widen, s + 2),
+                (square, s - 4),
+                (apply_taper, s - 3),
+                (scale_past, s),
+                (subtract, s - 1),
+                (quant_e, s - 3),
+                (quant_past, s),
+                (add, s - ADD_LAG),
+            )
+            if s % UNITS == 0 and 0 <= s and s // UNITS + AHEAD < BEAMS:
+                load_beam(s // UNITS + AHEAD)
+            for stage, i in plan:
+                if 0 <= i < STEPS:
+                    stage(i)
+            if s == 0:
+                spread_taper()

@@ -11,7 +11,9 @@ UNITS = PINGS // P
 STEPS = BEAMS * UNITS
 GROUPS = PAST // 512
 AHEAD = 2
-ADD_LAG = 4
+ADD_LAG = 5
+HEAD = 4
+LEAD = 3
 TAIL = 3
 
 F32 = mybir.dt.float32
@@ -66,12 +68,15 @@ def tile_reverb_prewhiten_replicas_s14_kernel(
             coef = inp.tile([P, GROUPS, 2 * NOW], U8, align_bytes=64)
             groups = slice(GROUPS * b, GROUPS * (b + 1))
             nc.sync.dma_start(out=coef[:].bitcast(I32), in_=coef_words[groups].rearrange("g p n -> p g n").bitcast(I32))
+            coefs[b] = coef
+
+        def load_coef_scales(b):
+            groups = slice(GROUPS * b, GROUPS * (b + 1))
             for r in range(4):
                 nc.sync.dma_start(
                     out=coef_s[b][r:P:32, :].rearrange("q (g n) -> q g n", g=GROUPS).bitcast(I32),
                     in_=coef_scales[groups, r:16:4, :].rearrange("g q n -> q g n").bitcast(I32),
                 )
-            coefs[b] = coef
 
         def load_bank(b):
             bank = inp.tile([P, 4 * DOPPLER], U8, align_bytes=64)
@@ -81,8 +86,10 @@ def tile_reverb_prewhiten_replicas_s14_kernel(
             banks[b] = bank
 
         def load_beam(b):
-            load_past(b, [slice(0, UNITS)])
+            if b + 1 < BEAMS:
+                load_past(b + 1, [slice(0, UNITS)])
             load_coef(b)
+            load_coef_scales(b)
             load_now(b)
             load_bank(b)
 
@@ -93,33 +100,39 @@ def tile_reverb_prewhiten_replicas_s14_kernel(
         nc.scalar.activation(out=ident16[:], in_=ident[:], func=ACT.Sqrt)
 
         nc.sync.dma_start(out=scale_sb[:], in_=past_scale.rearrange("a b (g p t) -> p (a b g) t", p=P, t=4))
-        load_past(0, [slice(0, 1), slice(1, UNITS)])
-        load_coef(0)
         nc.sync.dma_start(out=taper_sb[:], in_=taper.rearrange("b (p t) -> p b t", t=4))
+        load_past(0, [slice(0, 1), slice(1, UNITS)])
+        load_coef_scales(0)
+        load_coef(0)
+        load_past(1, [slice(0, UNITS)])
         load_now(0)
         load_bank(0)
-        for b in range(1, AHEAD):
-            load_beam(b)
 
         nc.vector.tensor_copy(out=scale_x[:], in_=scale_sb[:].unsqueeze(2).to_broadcast([P, GROUPS, P, 4]))
 
-        def spread_taper():
-            nc.vector.tensor_copy(
-                out=taper_x[:].bitcast(F32), in_=taper_sb[:].bitcast(F32).unsqueeze(2).to_broadcast([P, BEAMS, P, 2])
-            )
+        nc.vector.tensor_copy(
+            out=taper_x[:].bitcast(F32), in_=taper_sb[:].bitcast(F32).unsqueeze(2).to_broadcast([P, BEAMS, P, 2])
+        )
 
         raws, turned, groupeds, codes_p, preds, ds, dts, e16s, codes_e, ys, sqs, sums = ({} for k in range(12))
 
+        widened = []
+
         def vector_subtracts(i):
-            return i % 2 == 1 or i >= STEPS - TAIL
+            return (i % 5 in (1, 2, 4) and i >= HEAD) or i >= STEPS - TAIL
 
         def widen(i):
-            raw = work.tile([P, PAST], BF16, align_bytes=64)
+            raw = work.tile([P, PAST], BF16, align_bytes=64, bufs=LEAD + 3)
             nc.scalar.copy(out=raw[:], in_=pasts[i // UNITS][:, i % UNITS, :].bitcast(FP8))
             raws[i] = raw
 
+        def widen_ahead(s):
+            for i in range(len(widened), min(STEPS, s + 8 + min(max(s + 2, 0), LEAD))):
+                widen(i)
+                widened.append(i)
+
         def turn_past(i):
-            tp = psum2.tile([P, 2, GROUPS * P], F32)
+            tp = psum2.tile([P, 2, GROUPS * P], F32, tag="turn")
             words = raws.pop(i)[:].bitcast(F32)
             for g in range(GROUPS):
                 for u in range(2):
@@ -158,6 +171,14 @@ def tile_reverb_prewhiten_replicas_s14_kernel(
                 )
             preds[i] = pred
 
+        def subtract_on_scalar(i):
+            if not vector_subtracts(i):
+                subtract(i)
+
+        def subtract_on_vector(i):
+            if vector_subtracts(i):
+                subtract(i)
+
         def subtract(i):
             d = work.tile([P, 4, P], F32, align_bytes=64)
             pred = preds.pop(i)[:].rearrange("r (p t) -> r t p", t=4)
@@ -170,21 +191,21 @@ def tile_reverb_prewhiten_replicas_s14_kernel(
                 nc.scalar.activation(out=d[:], in_=pred, func=ACT.Copy, scale=-1.0)
             ds[i] = d
 
-        def turn_d(i):
+        def turn_now(i):
             dt = psum2.tile([P, 4, P], F32)
-            d = ds.pop(i)
-            now_u = nows[i // UNITS][:, i % UNITS, :]
-            if vector_subtracts(i):
-                for t in range(4):
-                    nc.tensor.transpose(dt[:, t, :], d[:, t, :], ident[:])
-            else:
+            if not vector_subtracts(i):
+                now_u = nows[i // UNITS][:, i % UNITS, :]
                 for t in range(4):
                     nc.tensor.matmul(dt[:, t, :], lhsT=now_u[:, t::4], rhs=ident16[:], start=(t == 0), stop=False)
-                for t in range(4):
-                    nc.tensor.matmul(
-                        dt[:, t, :], lhsT=d[:, t, :], rhs=ident[:], is_transpose=True, start=False, stop=(t == 3)
-                    )
             dts[i] = dt
+
+        def turn_d(i):
+            d = ds.pop(i)
+            alone = vector_subtracts(i)
+            for t in range(4):
+                nc.tensor.matmul(
+                    dts[i][:, t, :], lhsT=d[:, t, :], rhs=ident[:], is_transpose=True, start=alone, stop=alone or t == 3
+                )
 
         def apply_taper(i):
             e16 = work.tile([P, P, 4], BF16, align_bytes=64)
@@ -204,26 +225,41 @@ def tile_reverb_prewhiten_replicas_s14_kernel(
             )
             codes_e[i] = (ec, es)
 
+        def pieces(i):
+            if i == STEPS - 1:
+                return (slice(0, DOPPLER // 2), slice(DOPPLER // 2, DOPPLER))
+            return (slice(0, DOPPLER),)
+
         def correlate(i):
             b = i // UNITS
             ec, es = codes_e.pop(i)
-            y_i = psum1.tile([P, DOPPLER], F32)
-            y_q = psum1.tile([P, DOPPLER], F32)
-            for h, y in enumerate((y_i, y_q)):
+            if i >= STEPS - 4 and i % 2 == 0:
+                y_0 = psum2.tile([P, DOPPLER], F32, tag="turn")
+                y_1 = psum2.tile([P, DOPPLER], F32, tag="turn")
+            else:
+                y_0 = psum1.tile([P, DOPPLER], F32)
+                y_1 = psum1.tile([P, DOPPLER], F32)
+            if i == STEPS - 1:
+                parts = [(y, slice(256 * h, 256 * (h + 1)), DOPPLER * h + 256 * k) for k, y in enumerate((y_0, y_1)) for h in range(2)]
+            else:
+                parts = [(y, slice(0, DOPPLER), DOPPLER * h) for h, y in enumerate((y_0, y_1))]
+            for y, cols, first in parts:
+                width = cols.stop - cols.start
                 nc.tensor.matmul_mx(
-                    out=y[:],
+                    out=y[:, cols],
                     lhsT=ec[:].bitcast(FP8X4),
                     lhsT_scale=es[:],
-                    rhs=banks[b][:, 2 * DOPPLER * h : 2 * DOPPLER * (h + 1)].bitcast(FP4X4),
-                    rhs_scale=bank_s[b][:, DOPPLER * h : DOPPLER * (h + 1)],
+                    rhs=banks[b][:, 2 * first : 2 * (first + width)].bitcast(FP4X4),
+                    rhs_scale=bank_s[b][:, first : first + width],
                     start=True,
                     stop=True,
                 )
-            ys[i] = (y_i, y_q)
+            ys[i] = (y_0, y_1)
 
         def square(i):
             sq = work.tile([P, 2, DOPPLER], F32, align_bytes=64)
-            for h, y in enumerate(ys.pop(i)):
+            y_0, y_1 = ys.pop(i)
+            for h, y in ((0, y_0), (1, y_1)) if i >= STEPS - TAIL else ((1, y_1), (0, y_0)):
                 nc.scalar.activation(out=sq[:, h, :], in_=y[:], func=ACT.Square)
             sqs[i] = sq
 
@@ -235,36 +271,55 @@ def tile_reverb_prewhiten_replicas_s14_kernel(
             else:
                 total = work.tile([P, DOPPLER], F32, align_bytes=64)
                 power = total[:]
-                nc.vector.tensor_tensor(out=power, in0=sq[:, 0, :], in1=sq[:, 1, :], op=ALU.add)
+                if i == STEPS - 1:
+                    for k in range(2):
+                        nc.vector.tensor_tensor(
+                            out=power[:, 256 * k : 256 * (k + 1)], in0=sq[:, k, :256], in1=sq[:, k, 256:], op=ALU.add
+                        )
+                else:
+                    nc.vector.tensor_tensor(out=power, in0=sq[:, 0, :], in1=sq[:, 1, :], op=ALU.add)
             sums[i] = power
 
         def root(i):
             env = outs.tile([P, DOPPLER], F32, align_bytes=64)
-            nc.scalar.activation(out=env[:], in_=sums.pop(i), func=ACT.Sqrt)
-            nc.sync.dma_start(
-                out=out[i // UNITS].rearrange("(r j) d -> r j d", j=UNITS)[:, i % UNITS, :], in_=env[:]
-            )
+            power = sums.pop(i)
+            for cols in pieces(i):
+                nc.scalar.activation(out=env[:, cols], in_=power[:, cols], func=ACT.Sqrt)
+                nc.sync.dma_start(
+                    out=out[i // UNITS].rearrange("(r j) d -> r j d", j=UNITS)[:, i % UNITS, cols], in_=env[:, cols]
+                )
 
-        for s in range(-2, STEPS + 7):
+        for s in range(-7, STEPS + 3):
             plan = (
-                (correlate, s - 4),
-                (predict, s - 1),
-                (turn_d, s - 2),
-                (turn_past, s + 1),
-                (root, s - 6),
-                (widen, s + 2),
-                (square, s - 4),
-                (apply_taper, s - 3),
-                (scale_past, s),
-                (subtract, s - 1),
-                (quant_e, s - 3),
-                (quant_past, s),
-                (add, s - ADD_LAG),
+                (apply_taper, s),
+                (quant_past, s + 3),
+                (quant_e, s),
+                (add, s - 2),
+                (scale_past, s + 4),
+                (subtract, s + 2),
+                (correlate, s),
+                (predict, s + 3),
+                (square, s),
+                (root, s - 2),
+                (widen_ahead, s),
+                (turn_now, s + 2),
+                (turn_past, s + 6),
+                (turn_d, s + 2),
             )
-            if s % UNITS == 0 and 0 <= s and s // UNITS + AHEAD < BEAMS:
+            if s + 3 >= STEPS:
+                plan = (
+                    (apply_taper, s),
+                    (add, s - 2),
+                    (quant_e, s),
+                    (subtract, s + 2),
+                    (correlate, s),
+                    (root, s - 2),
+                    (square, s),
+                    (turn_now, s + 2),
+                    (turn_d, s + 2),
+                )
+            if s % UNITS == 0 and 1 <= s // UNITS + AHEAD < BEAMS:
                 load_beam(s // UNITS + AHEAD)
             for stage, i in plan:
-                if 0 <= i < STEPS:
+                if 0 <= i < STEPS or stage is widen_ahead:
                     stage(i)
-            if s == 0:
-                spread_taper()

@@ -10,10 +10,8 @@ P = 128
 UNITS = PINGS // P
 STEPS = BEAMS * UNITS
 GROUPS = PAST // 512
-AHEAD = 2
 ADD_LAG = 5
 HEAD = 4
-LEAD = 3
 TAIL = 3
 
 F32 = mybir.dt.float32
@@ -34,7 +32,7 @@ def tile_reverb_prewhiten_replicas_s14_kernel(
     nc = tc.nc
     with ExitStack() as ctx:
         keep = ctx.enter_context(tc.tile_pool(name="keep", bufs=1))
-        inp = ctx.enter_context(tc.tile_pool(name="inp", bufs=AHEAD + 2))
+        inp = ctx.enter_context(tc.tile_pool(name="inp", bufs=BEAMS))
         work = ctx.enter_context(tc.tile_pool(name="work", bufs=4))
         outs = ctx.enter_context(tc.tile_pool(name="outs", bufs=16))
         psum2 = ctx.enter_context(tc.psum_pool(name="psum2", bufs=2))
@@ -107,6 +105,8 @@ def tile_reverb_prewhiten_replicas_s14_kernel(
         load_past(1, [slice(0, UNITS)])
         load_now(0)
         load_bank(0)
+        for b in range(1, BEAMS):
+            load_beam(b)
 
         nc.vector.tensor_copy(out=scale_x[:], in_=scale_sb[:].unsqueeze(2).to_broadcast([P, GROUPS, P, 4]))
 
@@ -116,20 +116,13 @@ def tile_reverb_prewhiten_replicas_s14_kernel(
 
         raws, turned, groupeds, codes_p, preds, ds, dts, e16s, codes_e, ys, sqs, sums = ({} for k in range(12))
 
-        widened = []
-
         def vector_subtracts(i):
             return (i % 5 in (1, 2, 4) and i >= HEAD) or i >= STEPS - TAIL
 
         def widen(i):
-            raw = work.tile([P, PAST], BF16, align_bytes=64, bufs=LEAD + 3)
+            raw = work.tile([P, PAST], BF16, align_bytes=64, bufs=3)
             nc.scalar.copy(out=raw[:], in_=pasts[i // UNITS][:, i % UNITS, :].bitcast(FP8))
             raws[i] = raw
-
-        def widen_ahead(s):
-            for i in range(len(widened), min(STEPS, s + 8 + min(max(s + 2, 0), LEAD))):
-                widen(i)
-                widened.append(i)
 
         def turn_past(i):
             tp = psum2.tile([P, 2, GROUPS * P], F32, tag="turn")
@@ -259,7 +252,7 @@ def tile_reverb_prewhiten_replicas_s14_kernel(
         def square(i):
             sq = work.tile([P, 2, DOPPLER], F32, align_bytes=64)
             y_0, y_1 = ys.pop(i)
-            for h, y in ((0, y_0), (1, y_1)) if i >= STEPS - TAIL else ((1, y_1), (0, y_0)):
+            for h, y in enumerate((y_0, y_1)):
                 nc.scalar.activation(out=sq[:, h, :], in_=y[:], func=ACT.Square)
             sqs[i] = sq
 
@@ -301,7 +294,7 @@ def tile_reverb_prewhiten_replicas_s14_kernel(
                 (predict, s + 3),
                 (square, s),
                 (root, s - 2),
-                (widen_ahead, s),
+                (widen, s + 7),
                 (turn_now, s + 2),
                 (turn_past, s + 6),
                 (turn_d, s + 2),
@@ -318,8 +311,6 @@ def tile_reverb_prewhiten_replicas_s14_kernel(
                     (turn_now, s + 2),
                     (turn_d, s + 2),
                 )
-            if s % UNITS == 0 and 1 <= s // UNITS + AHEAD < BEAMS:
-                load_beam(s // UNITS + AHEAD)
             for stage, i in plan:
-                if 0 <= i < STEPS or stage is widen_ahead:
+                if 0 <= i < STEPS:
                     stage(i)

@@ -98,11 +98,11 @@ def tile_reverb_prewhiten_replicas_s14_kernel(
         nc.scalar.activation(out=ident16[:], in_=ident[:], func=ACT.Sqrt)
 
         nc.sync.dma_start(out=scale_sb[:], in_=past_scale.rearrange("a b (g p t) -> p (a b g) t", p=P, t=4))
-        nc.sync.dma_start(out=taper_sb[:], in_=taper.rearrange("b (p t) -> p b t", t=4))
         load_past(0, [slice(0, 1), slice(1, UNITS)])
-        load_coef_scales(0)
         load_coef(0)
+        load_coef_scales(0)
         load_past(1, [slice(0, UNITS)])
+        nc.sync.dma_start(out=taper_sb[:], in_=taper.rearrange("b (p t) -> p b t", t=4))
         load_now(0)
         load_bank(0)
         for b in range(1, BEAMS):
@@ -110,9 +110,12 @@ def tile_reverb_prewhiten_replicas_s14_kernel(
 
         nc.vector.tensor_copy(out=scale_x[:], in_=scale_sb[:].unsqueeze(2).to_broadcast([P, GROUPS, P, 4]))
 
-        nc.vector.tensor_copy(
-            out=taper_x[:].bitcast(F32), in_=taper_sb[:].bitcast(F32).unsqueeze(2).to_broadcast([P, BEAMS, P, 2])
-        )
+        def spread_taper(first):
+            half = slice(first, first + BEAMS // 2)
+            nc.scalar.copy(
+                out=taper_x[:, half].bitcast(F32),
+                in_=taper_sb[:, half].bitcast(F32).unsqueeze(2).to_broadcast([P, BEAMS // 2, P, 2]),
+            )
 
         raws, turned, groupeds, codes_p, preds, ds, dts, e16s, codes_e, ys, sqs, sums = ({} for k in range(12))
 
@@ -314,3 +317,5 @@ def tile_reverb_prewhiten_replicas_s14_kernel(
             for stage, i in plan:
                 if 0 <= i < STEPS:
                     stage(i)
+            if s in (-2, -1):
+                spread_taper((s + 2) * BEAMS // 2)

@@ -12,7 +12,8 @@ STEPS = BEAMS * UNITS
 GROUPS = PAST // 512
 ADD_LAG = 5
 HEAD = 4
-TAIL = 3
+CASTLESS = 6
+TAIL = 2
 
 F32 = mybir.dt.float32
 BF16 = mybir.dt.bfloat16
@@ -120,7 +121,7 @@ def tile_reverb_prewhiten_replicas_s14_kernel(
         raws, turned, groupeds, codes_p, preds, ds, dts, e16s, codes_e, ys, sqs, sums = ({} for k in range(12))
 
         def vector_subtracts(i):
-            return (i % 5 in (1, 2, 4) and i >= HEAD) or i >= STEPS - TAIL
+            return (i % 2 == 1 and HEAD <= i < STEPS - CASTLESS) or i >= STEPS - TAIL
 
         def widen(i):
             raw = work.tile([P, PAST], BF16, align_bytes=64, bufs=3)

@@ -11,7 +11,7 @@ UNITS = PINGS // P
 STEPS = BEAMS * UNITS
 GROUPS = PAST // 512
 ADD_LAG = 5
-HEAD = 4
+HEAD = 2
 CASTLESS = 6
 TAIL = 2
 
@@ -54,8 +54,8 @@ def tile_reverb_prewhiten_replicas_s14_kernel(
         def load_past(b, pieces):
             past_u8 = inp.tile([P, UNITS, PAST], U8, align_bytes=64)
             src = past_bytes[b].rearrange("(r j) k -> r j k", j=UNITS)
-            for piece in pieces:
-                nc.sync.dma_start(out=past_u8[:, piece, :], in_=src[:, piece, :])
+            for units, cols in pieces:
+                nc.sync.dma_start(out=past_u8[:, units, cols], in_=src[:, units, cols])
             pasts[b] = past_u8
 
         def load_now(b):
@@ -86,7 +86,7 @@ def tile_reverb_prewhiten_replicas_s14_kernel(
 
         def load_beam(b):
             if b + 1 < BEAMS:
-                load_past(b + 1, [slice(0, UNITS)])
+                load_past(b + 1, [(slice(0, UNITS), slice(0, PAST))])
             load_coef(b)
             load_coef_scales(b)
             load_now(b)
@@ -99,10 +99,10 @@ def tile_reverb_prewhiten_replicas_s14_kernel(
         nc.scalar.activation(out=ident16[:], in_=ident[:], func=ACT.Sqrt)
 
         nc.sync.dma_start(out=scale_sb[:], in_=past_scale.rearrange("a b (g p t) -> p (a b g) t", p=P, t=4))
-        load_past(0, [slice(0, 1), slice(1, UNITS)])
-        load_coef(0)
+        load_past(0, [(slice(0, 1), slice(0, 512)), (slice(0, 1), slice(512, PAST)), (slice(1, UNITS), slice(0, PAST))])
         load_coef_scales(0)
-        load_past(1, [slice(0, UNITS)])
+        load_coef(0)
+        load_past(1, [(slice(0, UNITS), slice(0, PAST))])
         nc.sync.dma_start(out=taper_sb[:], in_=taper.rearrange("b (p t) -> p b t", t=4))
         load_now(0)
         load_bank(0)
@@ -123,27 +123,40 @@ def tile_reverb_prewhiten_replicas_s14_kernel(
         def vector_subtracts(i):
             return (i % 2 == 1 and HEAD <= i < STEPS - CASTLESS) or i >= STEPS - TAIL
 
+        def spans(i):
+            return [range(g, g + 1) for g in range(GROUPS)] if i == 0 else [range(GROUPS)]
+
         def widen(i):
             raw = work.tile([P, PAST], BF16, align_bytes=64, bufs=3)
-            nc.scalar.copy(out=raw[:], in_=pasts[i // UNITS][:, i % UNITS, :].bitcast(FP8))
+            for groups in spans(i):
+                cols = slice(512 * groups.start, 512 * groups.stop)
+                nc.scalar.copy(out=raw[:, cols], in_=pasts[i // UNITS][:, i % UNITS, cols].bitcast(FP8))
             raws[i] = raw
 
         def turn_past(i):
-            tp = psum2.tile([P, 2, GROUPS * P], F32, tag="turn")
             words = raws.pop(i)[:].bitcast(F32)
-            for g in range(GROUPS):
-                for u in range(2):
-                    nc.tensor.transpose(tp[:, u, P * g : P * (g + 1)], words[:, 256 * g + u : 256 * (g + 1) : 2], ident[:])
-            turned[i] = tp
+            turned[i] = []
+            for groups in spans(i):
+                if groups.start == 0:
+                    tp = psum2.tile([P, 2, len(groups) * P], F32, tag="turn")
+                else:
+                    tp = psum1.tile([P, 2, len(groups) * P], F32, tag="y_1")
+                for n, g in enumerate(groups):
+                    for u in range(2):
+                        nc.tensor.transpose(
+                            tp[:, u, P * n : P * (n + 1)], words[:, 256 * g + u : 256 * (g + 1) : 2], ident[:]
+                        )
+                turned[i].append(tp)
 
         def scale_past(i):
             grouped = work.tile([P, PAST], BF16, align_bytes=64, bufs=6)
-            nc.vector.tensor_tensor(
-                out=grouped[:].rearrange("p (q u e) -> p q u e", u=2, e=2),
-                in0=scale_x[:].rearrange("p g r (u e) -> p (g r) u e", u=2),
-                in1=turned.pop(i)[:].bitcast(BF16).rearrange("p u (q e) -> p q u e", e=2),
-                op=ALU.mult,
-            )
+            for groups, tp in zip(spans(i), turned.pop(i)):
+                nc.vector.tensor_tensor(
+                    out=grouped[:, 512 * groups.start : 512 * groups.stop].rearrange("p (q u e) -> p q u e", u=2, e=2),
+                    in0=scale_x[:, groups.start : groups.stop].rearrange("p g r (u e) -> p (g r) u e", u=2),
+                    in1=tp[:].bitcast(BF16).rearrange("p u (q e) -> p q u e", e=2),
+                    op=ALU.mult,
+                )
             groupeds[i] = grouped
 
         def quant_past(i):
@@ -282,7 +295,8 @@ def tile_reverb_prewhiten_replicas_s14_kernel(
             power = sums.pop(i)
             for cols in pieces(i):
                 nc.scalar.activation(out=env[:, cols], in_=power[:, cols], func=ACT.Sqrt)
-                nc.sync.dma_start(
+                queue = nc.scalar if i == STEPS - 1 and cols.stop == DOPPLER else nc.sync
+                queue.dma_start(
                     out=out[i // UNITS].rearrange("(r j) d -> r j d", j=UNITS)[:, i % UNITS, cols], in_=env[:, cols]
                 )
 
@@ -315,6 +329,10 @@ def tile_reverb_prewhiten_replicas_s14_kernel(
                     (turn_now, s + 2),
                     (turn_d, s + 2),
                 )
+            if s == -2:
+                plan = tuple(step for step in plan if step[0] not in (quant_past, predict))
+            if s == -1:
+                plan = ((quant_past, 1), (predict, 1)) + plan
             for stage, i in plan:
                 if 0 <= i < STEPS:
                     stage(i)

@@ -10,6 +10,7 @@ P = 128
 UNITS = PINGS // P
 STEPS = BEAMS * UNITS
 GROUPS = PAST // 512
+SHARE = 512
 ADD_LAG = 5
 HEAD = 2
 CASTLESS = 6
@@ -121,16 +122,21 @@ def tile_reverb_prewhiten_replicas_s14_kernel(
         raws, turned, groupeds, codes_p, preds, ds, dts, e16s, codes_e, ys, sqs, sums = ({} for k in range(12))
 
         def vector_subtracts(i):
-            return (i % 2 == 1 and HEAD <= i < STEPS - CASTLESS) or i >= STEPS - TAIL
+            return (i % 7 in (1, 3, 5) and HEAD <= i < STEPS - CASTLESS) or i >= STEPS - TAIL
 
         def spans(i):
             return [range(g, g + 1) for g in range(GROUPS)] if i == 0 else [range(GROUPS)]
 
         def widen(i):
             raw = work.tile([P, PAST], BF16, align_bytes=64, bufs=3)
-            for groups in spans(i):
-                cols = slice(512 * groups.start, 512 * groups.stop)
-                nc.scalar.copy(out=raw[:, cols], in_=pasts[i // UNITS][:, i % UNITS, cols].bitcast(FP8))
+            codes = pasts[i // UNITS][:, i % UNITS, :]
+            if i >= 9 and vector_subtracts(i - 5):
+                nc.gpsimd.tensor_copy(out=raw[:, :SHARE], in_=codes[:, :SHARE].bitcast(FP8))
+                nc.scalar.copy(out=raw[:, SHARE:], in_=codes[:, SHARE:].bitcast(FP8))
+            else:
+                for groups in spans(i):
+                    cols = slice(512 * groups.start, 512 * groups.stop)
+                    nc.scalar.copy(out=raw[:, cols], in_=codes[:, cols].bitcast(FP8))
             raws[i] = raw
 
         def turn_past(i):

@@ -14,6 +14,14 @@ SHARE = 512
 ADD_LAG = 5
 HEAD = 2
 CASTLESS = 6
+PAST_AHEAD = 4
+PRELOAD = 4
+RAWS = 12
+SUBS = (5, 8, 11, 15, 18, 21, 24)
+EARLY = {-7: 1, -6: 2, -5: 4, -4: 4, -3: 6, -2: 9, -1: 12, 0: 14, 1: 16}
+LEAD = 15
+DONE = 24
+HEAD_UNITS = {3: 13, 4: 15}
 TAIL = 2
 
 F32 = mybir.dt.float32
@@ -36,7 +44,7 @@ def tile_reverb_prewhiten_replicas_s14_kernel(
         keep = ctx.enter_context(tc.tile_pool(name="keep", bufs=1))
         inp = ctx.enter_context(tc.tile_pool(name="inp", bufs=BEAMS))
         work = ctx.enter_context(tc.tile_pool(name="work", bufs=4))
-        outs = ctx.enter_context(tc.tile_pool(name="outs", bufs=16))
+        outs = ctx.enter_context(tc.tile_pool(name="outs", bufs=8))
         psum2 = ctx.enter_context(tc.psum_pool(name="psum2", bufs=2))
         psum1 = ctx.enter_context(tc.psum_pool(name="psum1", bufs=1))
         ctx.enter_context(tc.manual_schedule())
@@ -45,27 +53,31 @@ def tile_reverb_prewhiten_replicas_s14_kernel(
         bank_s = [keep.tile([P, 2 * DOPPLER], U8, align_bytes=64, name="bank_s%d" % b) for b in range(BEAMS)]
         scale_sb = keep.tile([P, GROUPS, 4], F32, align_bytes=64)
         scale_x = keep.tile([P, GROUPS, P, 4], F32, align_bytes=64)
-        taper_sb = keep.tile([P, BEAMS, 4], BF16, align_bytes=64)
-        taper_x = keep.tile([P, BEAMS, P, 4], BF16, align_bytes=64)
+        taper_rows = keep.tile([P, NOW], BF16, align_bytes=64)
+        taper_sb = keep.tile([P, BEAMS, 2], F32, align_bytes=64)
+        taper_0 = keep.tile([P, NOW], BF16, align_bytes=64)
         ident = keep.tile([P, P], F32, align_bytes=64)
         ident16 = keep.tile([P, P], BF16, align_bytes=64)
 
         pasts, nows, coefs, banks = {}, {}, {}, {}
 
+        whole = [(slice(0, UNITS), slice(0, PAST))]
+
         def load_past(b, pieces):
-            past_u8 = inp.tile([P, UNITS, PAST], U8, align_bytes=64)
+            if b not in pasts:
+                past_u8 = inp.tile([P, UNITS, PAST], U8, align_bytes=64)
+                pasts[b] = past_u8
             src = past_bytes[b].rearrange("(r j) k -> r j k", j=UNITS)
             for units, cols in pieces:
-                nc.sync.dma_start(out=past_u8[:, units, cols], in_=src[:, units, cols])
-            pasts[b] = past_u8
+                nc.sync.dma_start(out=pasts[b][:, units, cols], in_=src[:, units, cols])
 
         def load_now(b):
-            now_sb = inp.tile([P, UNITS, NOW], BF16, align_bytes=64)
+            now_sb = inp.tile([P, UNITS, NOW], BF16, align_bytes=64, bufs=PRELOAD + 1)
             nc.sync.dma_start(out=now_sb[:], in_=now[b].rearrange("(r j) n -> r j n", j=UNITS))
             nows[b] = now_sb
 
         def load_coef(b):
-            coef = inp.tile([P, GROUPS, 2 * NOW], U8, align_bytes=64)
+            coef = inp.tile([P, GROUPS, 2 * NOW], U8, align_bytes=64, bufs=PRELOAD + 1)
             groups = slice(GROUPS * b, GROUPS * (b + 1))
             nc.sync.dma_start(out=coef[:].bitcast(I32), in_=coef_words[groups].rearrange("g p n -> p g n").bitcast(I32))
             coefs[b] = coef
@@ -79,68 +91,98 @@ def tile_reverb_prewhiten_replicas_s14_kernel(
                 )
 
         def load_bank(b):
-            bank = inp.tile([P, 4 * DOPPLER], U8, align_bytes=64)
+            bank = inp.tile([P, 4 * DOPPLER], U8, align_bytes=64, bufs=PRELOAD + 1)
             nc.sync.dma_start(out=bank[:].bitcast(I32), in_=bank_words[b].bitcast(I32))
             for r in range(4):
                 nc.sync.dma_start(out=bank_s[b][r:P:32, :].bitcast(I32), in_=bank_scales[b, r:16:4, :].bitcast(I32))
             banks[b] = bank
 
         def load_beam(b):
-            if b + 1 < BEAMS:
-                load_past(b + 1, [(slice(0, UNITS), slice(0, PAST))])
-            load_coef(b)
             load_coef_scales(b)
+            load_coef(b)
             load_now(b)
+            if b + PAST_AHEAD < BEAMS:
+                load_past(b + PAST_AHEAD, whole)
             load_bank(b)
 
         make_identity(nc, ident[:])
+        nc.vector.memset(taper_rows[:].bitcast(F32), 0.0)
         for b in range(BEAMS):
             nc.vector.memset(coef_s[b][:].bitcast(I32), 0)
             nc.vector.memset(bank_s[b][:].bitcast(I32), 0)
         nc.scalar.activation(out=ident16[:], in_=ident[:], func=ACT.Sqrt)
 
+        load_past(0, [(slice(0, 1), slice(0, 512))])
         nc.sync.dma_start(out=scale_sb[:], in_=past_scale.rearrange("a b (g p t) -> p (a b g) t", p=P, t=4))
-        load_past(0, [(slice(0, 1), slice(0, 512)), (slice(0, 1), slice(512, PAST)), (slice(1, UNITS), slice(0, PAST))])
+        load_past(0, [(slice(0, 1), slice(512, PAST)), (slice(1, UNITS), slice(0, PAST))])
+        nc.sync.dma_start(out=taper_rows[0:BEAMS, :], in_=taper)
         load_coef_scales(0)
         load_coef(0)
-        load_past(1, [(slice(0, UNITS), slice(0, PAST))])
-        nc.sync.dma_start(out=taper_sb[:], in_=taper.rearrange("b (p t) -> p b t", t=4))
+        load_past(1, whole)
         load_now(0)
+        load_past(2, whole)
         load_bank(0)
-        for b in range(1, BEAMS):
+        for b in range(3, PAST_AHEAD + 1):
+            load_past(b, whole)
+        for b in range(1, PRELOAD):
             load_beam(b)
 
         nc.vector.tensor_copy(out=scale_x[:], in_=scale_sb[:].unsqueeze(2).to_broadcast([P, GROUPS, P, 4]))
 
-        def spread_taper(first):
-            half = slice(first, first + BEAMS // 2)
-            nc.scalar.copy(
-                out=taper_x[:, half].bitcast(F32),
-                in_=taper_sb[:, half].bitcast(F32).unsqueeze(2).to_broadcast([P, BEAMS // 2, P, 2]),
-            )
+        tapers = {}
 
+        def turn_taper():
+            tp = psum2.tile([P, 2, P], F32, tag="dt")
+            words = taper_rows[:].bitcast(F32)
+            for u in range(2):
+                nc.tensor.transpose(tp[:, u, :], words[:, u::2], ident[:])
+            nc.scalar.copy(out=taper_sb[:], in_=tp[:, :, 0:BEAMS].rearrange("p u b -> p b u"))
+
+        def spread_taper(beams, copy, home):
+            count = len(beams)
+            copy(
+                out=home[:, : NOW * count].bitcast(F32).rearrange("p (b r u) -> p b r u", b=count, u=2),
+                in_=taper_sb[:, beams.start : beams.stop, :].unsqueeze(2).to_broadcast([P, count, P, 2]),
+            )
+            for j, b in enumerate(beams):
+                tapers[b] = home[:, NOW * j : NOW * (j + 1)].rearrange("p (r t) -> p r t", t=4)
+
+        todo = [(i, h) for i in range(STEPS) for h in range(2)]
         raws, turned, groupeds, codes_p, preds, ds, dts, e16s, codes_e, ys, sqs, sums = ({} for k in range(12))
 
         def vector_subtracts(i):
-            return (i % 7 in (1, 3, 5) and HEAD <= i < STEPS - CASTLESS) or i >= STEPS - TAIL
+            return i in SUBS or i >= STEPS - TAIL
 
         def spans(i):
             return [range(g, g + 1) for g in range(GROUPS)] if i == 0 else [range(GROUPS)]
 
-        def widen(i):
-            raw = work.tile([P, PAST], BF16, align_bytes=64, bufs=3)
-            codes = pasts[i // UNITS][:, i % UNITS, :]
-            if i >= 9 and vector_subtracts(i - 5):
-                nc.gpsimd.tensor_copy(out=raw[:, :SHARE], in_=codes[:, :SHARE].bitcast(FP8))
-                nc.scalar.copy(out=raw[:, SHARE:], in_=codes[:, SHARE:].bitcast(FP8))
-            else:
-                for groups in spans(i):
-                    cols = slice(512 * groups.start, 512 * groups.stop)
-                    nc.scalar.copy(out=raw[:, cols], in_=codes[:, cols].bitcast(FP8))
-            raws[i] = raw
+        def widen(copy, i, halves, home=None):
+            if i not in raws:
+                if home is None:
+                    raw = work.tile([P, PAST], BF16, align_bytes=64, bufs=RAWS)
+                    home = raw[:]
+                raws[i] = home
+            cols = slice(512 * halves[0], 512 * (halves[-1] + 1))
+            copy(out=raws[i][:, cols], in_=pasts[i // UNITS][:, i % UNITS, cols].bitcast(FP8))
+            for h in halves:
+                todo.remove((i, h))
+
+        def widen_upto(units):
+            for i in range(min(units, STEPS)):
+                halves = [h for h in range(2) if (i, h) in todo]
+                if i == 0:
+                    for h in halves:
+                        widen(nc.scalar.copy, i, [h])
+                elif halves:
+                    widen(nc.scalar.copy, i, halves)
+
+        def help_widen(first, count, home=None):
+            later = [piece for piece in todo if piece[0] >= first][:count]
+            for i in sorted(set(i for i, h in later)):
+                widen(nc.gpsimd.tensor_copy, i, [h for j, h in later if j == i], home)
 
         def turn_past(i):
-            words = raws.pop(i)[:].bitcast(F32)
+            words = raws.pop(i).bitcast(F32)
             turned[i] = []
             for groups in spans(i):
                 if groups.start == 0:
@@ -155,7 +197,12 @@ def tile_reverb_prewhiten_replicas_s14_kernel(
                 turned[i].append(tp)
 
         def scale_past(i):
-            grouped = work.tile([P, PAST], BF16, align_bytes=64, bufs=6)
+            if i in (0, 2):
+                grouped = keep.tile([P, 2 * PAST], BF16, align_bytes=64, name="early%d" % i)
+            elif i in HEAD_UNITS:
+                grouped = keep.tile([P, PAST], BF16, align_bytes=64, name="early%d" % i)
+            else:
+                grouped = work.tile([P, PAST], BF16, align_bytes=64, bufs=6)
             for groups, tp in zip(spans(i), turned.pop(i)):
                 nc.vector.tensor_tensor(
                     out=grouped[:, 512 * groups.start : 512 * groups.stop].rearrange("p (q u e) -> p q u e", u=2, e=2),
@@ -168,7 +215,12 @@ def tile_reverb_prewhiten_replicas_s14_kernel(
         def quant_past(i):
             pc = work.tile([P, GROUPS * P], U32, align_bytes=64)
             ps = work.tile([P, GROUPS * P], U8, align_bytes=64)
-            nc.vector.quantize_mx(out=pc[:].bitcast(FP8X4), scales=ps[:], in_=groupeds[i][:])
+            nc.vector.quantize_mx(out=pc[:].bitcast(FP8X4), scales=ps[:], in_=groupeds[i][:, :PAST])
+            if i in (0, 2):
+                if i == 0:
+                    turn_taper()
+                    spread_taper(range(1), nc.scalar.copy, taper_0[:])
+                spread_taper(range(1, 5) if i == 0 else range(5, BEAMS), nc.gpsimd.tensor_copy, groupeds[i][:])
             codes_p[i] = (pc, ps)
 
         def predict(i):
@@ -208,7 +260,7 @@ def tile_reverb_prewhiten_replicas_s14_kernel(
             ds[i] = d
 
         def turn_now(i):
-            dt = psum2.tile([P, 4, P], F32)
+            dt = psum2.tile([P, 4, P], F32, tag="dt")
             if not vector_subtracts(i):
                 now_u = nows[i // UNITS][:, i % UNITS, :]
                 for t in range(4):
@@ -227,7 +279,7 @@ def tile_reverb_prewhiten_replicas_s14_kernel(
             e16 = work.tile([P, P, 4], BF16, align_bytes=64)
             nc.vector.tensor_tensor(
                 out=e16[:],
-                in0=taper_x[:, i // UNITS, :, :],
+                in0=tapers[i // UNITS],
                 in1=dts.pop(i)[:].rearrange("p t r -> p r t"),
                 op=ALU.mult,
             )
@@ -306,19 +358,30 @@ def tile_reverb_prewhiten_replicas_s14_kernel(
                     out=out[i // UNITS].rearrange("(r j) d -> r j d", j=UNITS)[:, i % UNITS, cols], in_=env[:, cols]
                 )
 
+        def helps(i):
+            if i in HEAD_UNITS:
+                help_widen(HEAD_UNITS[i], 2, groupeds.pop(i)[:])
+            elif i >= ADD_LAG and vector_subtracts(i - 1):
+                help_widen(i + 5, 1)
+
+        def casts(i):
+            s = i - 7
+            widen_upto(EARLY.get(s, max(i + 1, LEAD + (STEPS - LEAD) * s // DONE)))
+
         for s in range(-7, STEPS + 3):
             plan = (
                 (apply_taper, s),
                 (quant_past, s + 3),
                 (quant_e, s),
                 (add, s - 2),
+                (helps, s + 3),
                 (scale_past, s + 4),
                 (subtract, s + 2),
                 (correlate, s),
                 (predict, s + 3),
                 (square, s),
                 (root, s - 2),
-                (widen, s + 7),
+                (casts, s + 7),
                 (turn_now, s + 2),
                 (turn_past, s + 6),
                 (turn_d, s + 2),
@@ -342,5 +405,5 @@ def tile_reverb_prewhiten_replicas_s14_kernel(
             for stage, i in plan:
                 if 0 <= i < STEPS:
                     stage(i)
-            if s in (-2, -1):
-                spread_taper((s + 2) * BEAMS // 2)
+            if s >= UNITS and s % UNITS == 0 and s // UNITS + PRELOAD - 1 < BEAMS:
+                load_beam(s // UNITS + PRELOAD - 1)

@@ -16,12 +16,15 @@ HEAD = 2
 CASTLESS = 6
 PAST_AHEAD = 4
 PRELOAD = 4
-RAWS = 12
-SUBS = (5, 8, 11, 15, 18, 21, 24)
-EARLY = {-7: 1, -6: 2, -5: 4, -4: 4, -3: 6, -2: 9, -1: 12, 0: 14, 1: 16}
-LEAD = 15
+RAWS = 14
+SUBS = (4,7,9,12,14,17,19,22,25)
+EARLY = {-7: 1, -6: 2, -5: 4, -4: 4, -3: 7, -2: 10, -1: 13, 0: 15, 1: 17, 2: 19}
+LEAD = 17
 DONE = 24
-HEAD_UNITS = {3: 13, 4: 15}
+HEAD_UNITS = {3: 14, 4: 16}
+SORTS = (8,11,14,17,20,23,26)
+G_FIRST = 2
+TAPER_AT = -4
 TAIL = 2
 
 F32 = mybir.dt.float32
@@ -49,8 +52,8 @@ def tile_reverb_prewhiten_replicas_s14_kernel(
         psum1 = ctx.enter_context(tc.psum_pool(name="psum1", bufs=1))
         ctx.enter_context(tc.manual_schedule())
 
-        coef_s = [keep.tile([P, GROUPS * NOW], U8, align_bytes=64, name="coef_s%d" % b) for b in range(BEAMS)]
-        bank_s = [keep.tile([P, 2 * DOPPLER], U8, align_bytes=64, name="bank_s%d" % b) for b in range(BEAMS)]
+        coef_s = [keep.tile([P, GROUPS * NOW], U8, align_bytes=64, name="coef_s%d" % b) for b in range(PRELOAD)] * 2
+        bank_s = [keep.tile([P, 2 * DOPPLER], U8, align_bytes=64, name="bank_s%d" % b) for b in range(PRELOAD)] * 2
         scale_sb = keep.tile([P, GROUPS, 4], F32, align_bytes=64)
         scale_x = keep.tile([P, GROUPS, P, 4], F32, align_bytes=64)
         taper_rows = keep.tile([P, NOW], BF16, align_bytes=64)
@@ -107,17 +110,17 @@ def tile_reverb_prewhiten_replicas_s14_kernel(
 
         make_identity(nc, ident[:])
         nc.vector.memset(taper_rows[:].bitcast(F32), 0.0)
-        for b in range(BEAMS):
+        for b in range(PRELOAD):
             nc.vector.memset(coef_s[b][:].bitcast(I32), 0)
             nc.vector.memset(bank_s[b][:].bitcast(I32), 0)
         nc.scalar.activation(out=ident16[:], in_=ident[:], func=ACT.Sqrt)
 
         load_past(0, [(slice(0, 1), slice(0, 512))])
         nc.sync.dma_start(out=scale_sb[:], in_=past_scale.rearrange("a b (g p t) -> p (a b g) t", p=P, t=4))
-        load_past(0, [(slice(0, 1), slice(512, PAST)), (slice(1, UNITS), slice(0, PAST))])
+        load_past(0, [(slice(0, 1), slice(512, PAST)), (slice(1, 2), slice(0, PAST)), (slice(2, UNITS), slice(0, PAST))])
+        load_coef(0)
         nc.sync.dma_start(out=taper_rows[0:BEAMS, :], in_=taper)
         load_coef_scales(0)
-        load_coef(0)
         load_past(1, whole)
         load_now(0)
         load_past(2, whole)
@@ -129,7 +132,7 @@ def tile_reverb_prewhiten_replicas_s14_kernel(
 
         nc.vector.tensor_copy(out=scale_x[:], in_=scale_sb[:].unsqueeze(2).to_broadcast([P, GROUPS, P, 4]))
 
-        tapers = {}
+        tapers, sorteds = {}, {}
 
         def turn_taper():
             tp = psum2.tile([P, 2, P], F32, tag="dt")
@@ -181,19 +184,26 @@ def tile_reverb_prewhiten_replicas_s14_kernel(
             for i in sorted(set(i for i, h in later)):
                 widen(nc.gpsimd.tensor_copy, i, [h for j, h in later if j == i], home)
 
+        def sort_past(i):
+            if i in SORTS:
+                ordered = work.tile([P, GROUPS, 2, P], F32, align_bytes=64, bufs=3)
+                nc.scalar.copy(out=ordered[:], in_=raws[i].bitcast(F32).rearrange("r (g p u) -> r g u p", g=GROUPS, u=2))
+                sorteds[i] = ordered
+
         def turn_past(i):
             words = raws.pop(i).bitcast(F32)
             turned[i] = []
             for groups in spans(i):
-                if groups.start == 0:
+                if i == 3:
+                    tp = psum1.tile([P, 2, len(groups) * P], F32, tag="y_0")
+                elif groups.start == 0:
                     tp = psum2.tile([P, 2, len(groups) * P], F32, tag="turn")
                 else:
                     tp = psum1.tile([P, 2, len(groups) * P], F32, tag="y_1")
                 for n, g in enumerate(groups):
                     for u in range(2):
-                        nc.tensor.transpose(
-                            tp[:, u, P * n : P * (n + 1)], words[:, 256 * g + u : 256 * (g + 1) : 2], ident[:]
-                        )
+                        source = sorteds[i][:, g, u, :] if i in SORTS else words[:, 256 * g + u : 256 * (g + 1) : 2]
+                        nc.tensor.transpose(tp[:, u, P * n : P * (n + 1)], source, ident[:])
                 turned[i].append(tp)
 
         def scale_past(i):
@@ -217,9 +227,6 @@ def tile_reverb_prewhiten_replicas_s14_kernel(
             ps = work.tile([P, GROUPS * P], U8, align_bytes=64)
             nc.vector.quantize_mx(out=pc[:].bitcast(FP8X4), scales=ps[:], in_=groupeds[i][:, :PAST])
             if i in (0, 2):
-                if i == 0:
-                    turn_taper()
-                    spread_taper(range(1), nc.scalar.copy, taper_0[:])
                 spread_taper(range(1, 5) if i == 0 else range(5, BEAMS), nc.gpsimd.tensor_copy, groupeds[i][:])
             codes_p[i] = (pc, ps)
 
@@ -382,6 +389,7 @@ def tile_reverb_prewhiten_replicas_s14_kernel(
                 (square, s),
                 (root, s - 2),
                 (casts, s + 7),
+                (sort_past, s + 7),
                 (turn_now, s + 2),
                 (turn_past, s + 6),
                 (turn_d, s + 2),
@@ -398,10 +406,19 @@ def tile_reverb_prewhiten_replicas_s14_kernel(
                     (turn_now, s + 2),
                     (turn_d, s + 2),
                 )
+            if s == -4:
+                plan = plan + ((turn_past, 3),)
+            if s == -3:
+                plan = ((scale_past, 1), (quant_past, 0), (helps, 0), (predict, 0), (casts, 4))
             if s == -2:
                 plan = tuple(step for step in plan if step[0] not in (quant_past, predict))
             if s == -1:
                 plan = ((quant_past, 1), (predict, 1)) + plan
+            if s == -6 and G_FIRST:
+                help_widen(G_FIRST, 2)
+            if s == TAPER_AT:
+                turn_taper()
+                spread_taper(range(1), nc.scalar.copy, taper_0[:])
             for stage, i in plan:
                 if 0 <= i < STEPS:
                     stage(i)

@@ -266,21 +266,26 @@ def tile_reverb_prewhiten_replicas_s14_kernel(
                 nc.scalar.activation(out=d[:], in_=pred, func=ACT.Copy, scale=-1.0)
             ds[i] = d
 
+        def add_now(i, slots):
+            now_u = nows[i // UNITS][:, i % UNITS, :]
+            for t in slots:
+                nc.tensor.matmul(dts[i][:, t, :], lhsT=now_u[:, t::4], rhs=ident16[:], start=(t == 0), stop=(t == 3))
+
         def turn_now(i):
             dt = psum2.tile([P, 4, P], F32, tag="dt")
-            if not vector_subtracts(i):
-                now_u = nows[i // UNITS][:, i % UNITS, :]
-                for t in range(4):
-                    nc.tensor.matmul(dt[:, t, :], lhsT=now_u[:, t::4], rhs=ident16[:], start=(t == 0), stop=False)
             dts[i] = dt
+            if not vector_subtracts(i):
+                add_now(i, range(2))
 
         def turn_d(i):
             d = ds.pop(i)
             alone = vector_subtracts(i)
             for t in range(4):
                 nc.tensor.matmul(
-                    dts[i][:, t, :], lhsT=d[:, t, :], rhs=ident[:], is_transpose=True, start=alone, stop=alone or t == 3
+                    dts[i][:, t, :], lhsT=d[:, t, :], rhs=ident[:], is_transpose=True, start=alone, stop=alone
                 )
+            if not alone:
+                add_now(i, range(2, 4))
 
         def apply_taper(i):
             e16 = work.tile([P, P, 4], BF16, align_bytes=64)

@@ -17,12 +17,12 @@ CASTLESS = 6
 PAST_AHEAD = 4
 PRELOAD = 4
 RAWS = 14
-SUBS = (4,7,9,12,14,17,19,22,25)
+SUBS = (5, 8, 11, 15, 18, 21, 24)
 EARLY = {-7: 1, -6: 2, -5: 4, -4: 4, -3: 7, -2: 10, -1: 13, 0: 15, 1: 17, 2: 19}
 LEAD = 17
 DONE = 24
 HEAD_UNITS = {3: 14, 4: 16}
-SORTS = (8,11,14,17,20,23,26)
+SORTS = ()
 G_FIRST = 2
 TAPER_AT = -4
 TAIL = 2

@@ -10,22 +10,14 @@ P = 128
 UNITS = PINGS // P
 STEPS = BEAMS * UNITS
 GROUPS = PAST // 512
-SHARE = 512
+HALF = PAST // 2
 ADD_LAG = 5
-HEAD = 2
-CASTLESS = 6
-PAST_AHEAD = 4
-PRELOAD = 4
-RAWS = 14
-SUBS = (5, 8, 11, 15, 18, 21, 24)
-EARLY = {-7: 1, -6: 2, -5: 4, -4: 4, -3: 7, -2: 10, -1: 13, 0: 15, 1: 17, 2: 19}
-LEAD = 17
-DONE = 24
-HEAD_UNITS = {3: 14, 4: 16}
-SORTS = ()
-G_FIRST = 2
-TAPER_AT = -4
+HELD = 4
 TAIL = 2
+CASTLESS = 6
+FILL_CASTS = 3
+LEAD = 17
+RAWS = 14
 
 F32 = mybir.dt.float32
 BF16 = mybir.dt.bfloat16
@@ -52,8 +44,8 @@ def tile_reverb_prewhiten_replicas_s14_kernel(
         psum1 = ctx.enter_context(tc.psum_pool(name="psum1", bufs=1))
         ctx.enter_context(tc.manual_schedule())
 
-        coef_s = [keep.tile([P, GROUPS * NOW], U8, align_bytes=64, name="coef_s%d" % b) for b in range(PRELOAD)] * 2
-        bank_s = [keep.tile([P, 2 * DOPPLER], U8, align_bytes=64, name="bank_s%d" % b) for b in range(PRELOAD)] * 2
+        coef_s = [keep.tile([P, GROUPS * NOW], U8, align_bytes=64, name="coef_s%d" % b) for b in range(HELD)] * 2
+        bank_s = [keep.tile([P, 2 * DOPPLER], U8, align_bytes=64, name="bank_s%d" % b) for b in range(HELD)] * 2
         scale_sb = keep.tile([P, GROUPS, 4], F32, align_bytes=64)
         scale_x = keep.tile([P, GROUPS, P, 4], F32, align_bytes=64)
         taper_rows = keep.tile([P, NOW], BF16, align_bytes=64)
@@ -75,12 +67,12 @@ def tile_reverb_prewhiten_replicas_s14_kernel(
                 nc.sync.dma_start(out=pasts[b][:, units, cols], in_=src[:, units, cols])
 
         def load_now(b):
-            now_sb = inp.tile([P, UNITS, NOW], BF16, align_bytes=64, bufs=PRELOAD + 1)
+            now_sb = inp.tile([P, UNITS, NOW], BF16, align_bytes=64, bufs=HELD + 1)
             nc.sync.dma_start(out=now_sb[:], in_=now[b].rearrange("(r j) n -> r j n", j=UNITS))
             nows[b] = now_sb
 
         def load_coef(b):
-            coef = inp.tile([P, GROUPS, 2 * NOW], U8, align_bytes=64, bufs=PRELOAD + 1)
+            coef = inp.tile([P, GROUPS, 2 * NOW], U8, align_bytes=64, bufs=HELD + 1)
             groups = slice(GROUPS * b, GROUPS * (b + 1))
             nc.sync.dma_start(out=coef[:].bitcast(I32), in_=coef_words[groups].rearrange("g p n -> p g n").bitcast(I32))
             coefs[b] = coef
@@ -94,7 +86,7 @@ def tile_reverb_prewhiten_replicas_s14_kernel(
                 )
 
         def load_bank(b):
-            bank = inp.tile([P, 4 * DOPPLER], U8, align_bytes=64, bufs=PRELOAD + 1)
+            bank = inp.tile([P, 4 * DOPPLER], U8, align_bytes=64, bufs=HELD + 1)
             nc.sync.dma_start(out=bank[:].bitcast(I32), in_=bank_words[b].bitcast(I32))
             for r in range(4):
                 nc.sync.dma_start(out=bank_s[b][r:P:32, :].bitcast(I32), in_=bank_scales[b, r:16:4, :].bitcast(I32))
@@ -104,13 +96,13 @@ def tile_reverb_prewhiten_replicas_s14_kernel(
             load_coef_scales(b)
             load_coef(b)
             load_now(b)
-            if b + PAST_AHEAD < BEAMS:
-                load_past(b + PAST_AHEAD, whole)
+            if b + HELD < BEAMS:
+                load_past(b + HELD, whole)
             load_bank(b)
 
         make_identity(nc, ident[:])
         nc.vector.memset(taper_rows[:].bitcast(F32), 0.0)
-        for b in range(PRELOAD):
+        for b in range(HELD):
             nc.vector.memset(coef_s[b][:].bitcast(I32), 0)
             nc.vector.memset(bank_s[b][:].bitcast(I32), 0)
         nc.scalar.activation(out=ident16[:], in_=ident[:], func=ACT.Sqrt)
@@ -125,14 +117,15 @@ def tile_reverb_prewhiten_replicas_s14_kernel(
         load_now(0)
         load_past(2, whole)
         load_bank(0)
-        for b in range(3, PAST_AHEAD + 1):
+        for b in range(3, HELD + 1):
             load_past(b, whole)
-        for b in range(1, PRELOAD):
+        for b in range(1, HELD):
             load_beam(b)
 
-        nc.vector.tensor_copy(out=scale_x[:], in_=scale_sb[:].unsqueeze(2).to_broadcast([P, GROUPS, P, 4]))
+        for g in range(GROUPS):
+            nc.vector.tensor_copy(out=scale_x[:, g], in_=scale_sb[:, g : g + 1, :].to_broadcast([P, P, 4]))
 
-        tapers, sorteds = {}, {}
+        tapers = {}
 
         def turn_taper():
             tp = psum2.tile([P, 2, P], F32, tag="dt")
@@ -154,7 +147,7 @@ def tile_reverb_prewhiten_replicas_s14_kernel(
         raws, turned, groupeds, codes_p, preds, ds, dts, e16s, codes_e, ys, sqs, sums = ({} for k in range(12))
 
         def vector_subtracts(i):
-            return i in SUBS or i >= STEPS - TAIL
+            return (i % UNITS == 0 and 0 < i < STEPS - CASTLESS) or i >= STEPS - TAIL
 
         def spans(i):
             return [range(g, g + 1) for g in range(GROUPS)] if i == 0 else [range(GROUPS)]
@@ -165,7 +158,7 @@ def tile_reverb_prewhiten_replicas_s14_kernel(
                     raw = work.tile([P, PAST], BF16, align_bytes=64, bufs=RAWS)
                     home = raw[:]
                 raws[i] = home
-            cols = slice(512 * halves[0], 512 * (halves[-1] + 1))
+            cols = slice(HALF * halves[0], HALF * (halves[-1] + 1))
             copy(out=raws[i][:, cols], in_=pasts[i // UNITS][:, i % UNITS, cols].bitcast(FP8))
             for h in halves:
                 todo.remove((i, h))
@@ -184,12 +177,6 @@ def tile_reverb_prewhiten_replicas_s14_kernel(
             for i in sorted(set(i for i, h in later)):
                 widen(nc.gpsimd.tensor_copy, i, [h for j, h in later if j == i], home)
 
-        def sort_past(i):
-            if i in SORTS:
-                ordered = work.tile([P, GROUPS, 2, P], F32, align_bytes=64, bufs=3)
-                nc.scalar.copy(out=ordered[:], in_=raws[i].bitcast(F32).rearrange("r (g p u) -> r g u p", g=GROUPS, u=2))
-                sorteds[i] = ordered
-
         def turn_past(i):
             words = raws.pop(i).bitcast(F32)
             turned[i] = []
@@ -202,14 +189,15 @@ def tile_reverb_prewhiten_replicas_s14_kernel(
                     tp = psum1.tile([P, 2, len(groups) * P], F32, tag="y_1")
                 for n, g in enumerate(groups):
                     for u in range(2):
-                        source = sorteds[i][:, g, u, :] if i in SORTS else words[:, 256 * g + u : 256 * (g + 1) : 2]
-                        nc.tensor.transpose(tp[:, u, P * n : P * (n + 1)], source, ident[:])
+                        nc.tensor.transpose(
+                            tp[:, u, P * n : P * (n + 1)], words[:, 256 * g + u : 256 * (g + 1) : 2], ident[:]
+                        )
                 turned[i].append(tp)
 
         def scale_past(i):
             if i in (0, 2):
                 grouped = keep.tile([P, 2 * PAST], BF16, align_bytes=64, name="early%d" % i)
-            elif i in HEAD_UNITS:
+            elif i < ADD_LAG and i != 1:
                 grouped = keep.tile([P, PAST], BF16, align_bytes=64, name="early%d" % i)
             else:
                 grouped = work.tile([P, PAST], BF16, align_bytes=64, bufs=6)
@@ -227,7 +215,7 @@ def tile_reverb_prewhiten_replicas_s14_kernel(
             ps = work.tile([P, GROUPS * P], U8, align_bytes=64)
             nc.vector.quantize_mx(out=pc[:].bitcast(FP8X4), scales=ps[:], in_=groupeds[i][:, :PAST])
             if i in (0, 2):
-                spread_taper(range(1, 5) if i == 0 else range(5, BEAMS), nc.gpsimd.tensor_copy, groupeds[i][:])
+                spread_taper(range(1, 4) if i == 0 else range(4, BEAMS), nc.gpsimd.tensor_copy, groupeds[i][:])
             codes_p[i] = (pc, ps)
 
         def predict(i):
@@ -245,14 +233,6 @@ def tile_reverb_prewhiten_replicas_s14_kernel(
                     stop=(g == GROUPS - 1),
                 )
             preds[i] = pred
-
-        def subtract_on_scalar(i):
-            if not vector_subtracts(i):
-                subtract(i)
-
-        def subtract_on_vector(i):
-            if vector_subtracts(i):
-                subtract(i)
 
         def subtract(i):
             d = work.tile([P, 4, P], F32, align_bytes=64)
@@ -371,14 +351,18 @@ def tile_reverb_prewhiten_replicas_s14_kernel(
                 )
 
         def helps(i):
-            if i in HEAD_UNITS:
-                help_widen(HEAD_UNITS[i], 2, groupeds.pop(i)[:])
+            if 2 < i < ADD_LAG:
+                help_widen(0, 2, groupeds.pop(i)[:])
             elif i >= ADD_LAG and vector_subtracts(i - 1):
                 help_widen(i + 5, 1)
 
         def casts(i):
             s = i - 7
-            widen_upto(EARLY.get(s, max(i + 1, LEAD + (STEPS - LEAD) * s // DONE)))
+            if s < -3:
+                widen_upto(min(i + 1 + i // 2, UNITS))
+            else:
+                even = LEAD + (STEPS - LEAD) * s // (STEPS - 8)
+                widen_upto(max(i + 1, min(FILL_CASTS * (s + 5), even)))
 
         for s in range(-7, STEPS + 3):
             plan = (
@@ -394,7 +378,6 @@ def tile_reverb_prewhiten_replicas_s14_kernel(
                 (square, s),
                 (root, s - 2),
                 (casts, s + 7),
-                (sort_past, s + 7),
                 (turn_now, s + 2),
                 (turn_past, s + 6),
                 (turn_d, s + 2),
@@ -411,21 +394,19 @@ def tile_reverb_prewhiten_replicas_s14_kernel(
                     (turn_now, s + 2),
                     (turn_d, s + 2),
                 )
-            if s == -4:
-                plan = plan + ((turn_past, 3),)
             if s == -3:
-                plan = ((scale_past, 1), (quant_past, 0), (helps, 0), (predict, 0), (casts, 4))
+                plan = ((quant_past, 0), (scale_past, 1), (helps, 0), (predict, 0), (casts, 4), (turn_past, 3))
             if s == -2:
                 plan = tuple(step for step in plan if step[0] not in (quant_past, predict))
             if s == -1:
                 plan = ((quant_past, 1), (predict, 1)) + plan
-            if s == -6 and G_FIRST:
-                help_widen(G_FIRST, 2)
-            if s == TAPER_AT:
+            if s == -6:
+                help_widen(UNITS - 1, 2)
+            if s == -4:
                 turn_taper()
                 spread_taper(range(1), nc.scalar.copy, taper_0[:])
             for stage, i in plan:
                 if 0 <= i < STEPS:
                     stage(i)
-            if s >= UNITS and s % UNITS == 0 and s // UNITS + PRELOAD - 1 < BEAMS:
-                load_beam(s // UNITS + PRELOAD - 1)
+            if s >= UNITS and s % UNITS == 0 and s // UNITS + HELD - 1 < BEAMS:
+                load_beam(s // UNITS + HELD - 1)

@@ -10,14 +10,16 @@ P = 128
 UNITS = PINGS // P
 STEPS = BEAMS * UNITS
 GROUPS = PAST // 512
-HALF = PAST // 2
 ADD_LAG = 5
 HELD = 4
 TAIL = 2
-CASTLESS = 6
-FILL_CASTS = 3
-LEAD = 17
-RAWS = 14
+EVERY = 5
+LONG_CAST = 640
+LEAD = 20
+CAST_STEPS = 22
+RAWS = 16
+H1, H2, H3 = 9, 14, 18
+REP = 8
 
 F32 = mybir.dt.float32
 BF16 = mybir.dt.bfloat16
@@ -41,7 +43,7 @@ def tile_reverb_prewhiten_replicas_s14_kernel(
         work = ctx.enter_context(tc.tile_pool(name="work", bufs=4))
         outs = ctx.enter_context(tc.tile_pool(name="outs", bufs=8))
         psum2 = ctx.enter_context(tc.psum_pool(name="psum2", bufs=2))
-        psum1 = ctx.enter_context(tc.psum_pool(name="psum1", bufs=1))
+        psum4 = ctx.enter_context(tc.psum_pool(name="psum4", bufs=4))
         ctx.enter_context(tc.manual_schedule())
 
         coef_s = [keep.tile([P, GROUPS * NOW], U8, align_bytes=64, name="coef_s%d" % b) for b in range(HELD)] * 2
@@ -49,13 +51,11 @@ def tile_reverb_prewhiten_replicas_s14_kernel(
         scale_sb = keep.tile([P, GROUPS, 4], F32, align_bytes=64)
         scale_x = keep.tile([P, GROUPS, P, 4], F32, align_bytes=64)
         taper_rows = keep.tile([P, NOW], BF16, align_bytes=64)
-        taper_sb = keep.tile([P, BEAMS, 2], F32, align_bytes=64)
-        taper_0 = keep.tile([P, NOW], BF16, align_bytes=64)
+        taper_x = keep.tile([P, BEAMS, REP, 4], BF16, align_bytes=64)
         ident = keep.tile([P, P], F32, align_bytes=64)
-        ident16 = keep.tile([P, P], BF16, align_bytes=64)
+        minus16 = keep.tile([P, P], BF16, align_bytes=64)
 
         pasts, nows, coefs, banks = {}, {}, {}, {}
-
         whole = [(slice(0, UNITS), slice(0, PAST))]
 
         def load_past(b, pieces):
@@ -105,88 +105,78 @@ def tile_reverb_prewhiten_replicas_s14_kernel(
         for b in range(HELD):
             nc.vector.memset(coef_s[b][:].bitcast(I32), 0)
             nc.vector.memset(bank_s[b][:].bitcast(I32), 0)
-        nc.scalar.activation(out=ident16[:], in_=ident[:], func=ACT.Sqrt)
+        nc.scalar.activation(out=minus16[:], in_=ident[:], func=ACT.Sqrt)
+        nc.vector.tensor_scalar(out=minus16[:], in0=minus16[:], scalar1=-1.0, scalar2=None, op0=ALU.mult)
 
         load_past(0, [(slice(0, 1), slice(0, 512))])
         nc.sync.dma_start(out=scale_sb[:], in_=past_scale.rearrange("a b (g p t) -> p (a b g) t", p=P, t=4))
         load_past(0, [(slice(0, 1), slice(512, PAST)), (slice(1, 2), slice(0, PAST)), (slice(2, UNITS), slice(0, PAST))])
-        load_coef(0)
-        nc.sync.dma_start(out=taper_rows[0:BEAMS, :], in_=taper)
-        load_coef_scales(0)
         load_past(1, whole)
-        load_now(0)
+        nc.sync.dma_start(out=taper_rows[0:BEAMS, :], in_=taper)
+        load_coef(0)
+        load_coef_scales(0)
         load_past(2, whole)
+        load_now(0)
+        load_past(3, whole)
         load_bank(0)
-        for b in range(3, HELD + 1):
-            load_past(b, whole)
+        load_past(HELD, whole)
         for b in range(1, HELD):
             load_beam(b)
 
         for g in range(GROUPS):
             nc.vector.tensor_copy(out=scale_x[:, g], in_=scale_sb[:, g : g + 1, :].to_broadcast([P, P, 4]))
 
-        tapers = {}
-
         def turn_taper():
             tp = psum2.tile([P, 2, P], F32, tag="dt")
             words = taper_rows[:].bitcast(F32)
             for u in range(2):
                 nc.tensor.transpose(tp[:, u, :], words[:, u::2], ident[:])
-            nc.scalar.copy(out=taper_sb[:], in_=tp[:, :, 0:BEAMS].rearrange("p u b -> p b u"))
-
-        def spread_taper(beams, copy, home):
-            count = len(beams)
-            copy(
-                out=home[:, : NOW * count].bitcast(F32).rearrange("p (b r u) -> p b r u", b=count, u=2),
-                in_=taper_sb[:, beams.start : beams.stop, :].unsqueeze(2).to_broadcast([P, count, P, 2]),
+            nc.scalar.activation(
+                out=taper_x[:, :, 0, :].rearrange("p b (u e) -> p b u e", u=2),
+                in_=tp[:].bitcast(BF16)[:, :, : 2 * BEAMS].rearrange("p u (b e) -> p b u e", e=2),
+                func=ACT.Copy,
+                scale=-1.0,
             )
-            for j, b in enumerate(beams):
-                tapers[b] = home[:, NOW * j : NOW * (j + 1)].rearrange("p (r t) -> p r t", t=4)
 
-        todo = [(i, h) for i in range(STEPS) for h in range(2)]
+        def spread_taper():
+            words = taper_x[:].bitcast(F32)
+            nc.scalar.copy(out=words[:, :, 1:, :], in_=words[:, :, 0:1, :].to_broadcast([P, BEAMS, REP - 1, 2]))
+
+        cast = [0] * STEPS
         raws, turned, groupeds, codes_p, preds, ds, dts, e16s, codes_e, ys, sqs, sums = ({} for k in range(12))
 
         def vector_subtracts(i):
-            return (i % UNITS == 0 and 0 < i < STEPS - CASTLESS) or i >= STEPS - TAIL
+            return (i % EVERY == EVERY - 1 and i < STEPS - ADD_LAG) or i >= STEPS - TAIL
+
+        def early_for_gpsimd(i):
+            return i % UNITS == UNITS - 1 and i < LEAD
 
         def spans(i):
             return [range(g, g + 1) for g in range(GROUPS)] if i == 0 else [range(GROUPS)]
 
-        def widen(copy, i, halves, home=None):
+        def widen(copy, i, count, home=None):
             if i not in raws:
                 if home is None:
                     raw = work.tile([P, PAST], BF16, align_bytes=64, bufs=RAWS)
                     home = raw[:]
                 raws[i] = home
-            cols = slice(HALF * halves[0], HALF * (halves[-1] + 1))
+            cols = slice(cast[i], min(cast[i] + count, PAST))
             copy(out=raws[i][:, cols], in_=pasts[i // UNITS][:, i % UNITS, cols].bitcast(FP8))
-            for h in halves:
-                todo.remove((i, h))
+            cast[i] = cols.stop
 
         def widen_upto(units):
             for i in range(min(units, STEPS)):
-                halves = [h for h in range(2) if (i, h) in todo]
-                if i == 0:
-                    for h in halves:
-                        widen(nc.scalar.copy, i, [h])
-                elif halves:
-                    widen(nc.scalar.copy, i, halves)
-
-        def help_widen(first, count, home=None):
-            later = [piece for piece in todo if piece[0] >= first][:count]
-            for i in sorted(set(i for i, h in later)):
-                widen(nc.gpsimd.tensor_copy, i, [h for j, h in later if j == i], home)
+                while cast[i] < PAST and not early_for_gpsimd(i):
+                    widen(nc.scalar.copy, i, 512 if i == 0 else PAST)
 
         def turn_past(i):
             words = raws.pop(i).bitcast(F32)
             turned[i] = []
             for groups in spans(i):
-                if i == 3:
-                    tp = psum1.tile([P, 2, len(groups) * P], F32, tag="y_0")
-                elif groups.start == 0:
-                    tp = psum2.tile([P, 2, len(groups) * P], F32, tag="turn")
+                if i == 3 or groups.start > 0:
+                    tp = psum4.tile([P, 2, len(groups) * P], F32, tag="mx")
                 else:
-                    tp = psum1.tile([P, 2, len(groups) * P], F32, tag="y_1")
+                    tp = psum2.tile([P, 2, len(groups) * P], F32, tag="turn")
                 for n, g in enumerate(groups):
                     for u in range(2):
                         nc.tensor.transpose(
@@ -195,9 +185,7 @@ def tile_reverb_prewhiten_replicas_s14_kernel(
                 turned[i].append(tp)
 
         def scale_past(i):
-            if i in (0, 2):
-                grouped = keep.tile([P, 2 * PAST], BF16, align_bytes=64, name="early%d" % i)
-            elif i < ADD_LAG and i != 1:
+            if i < ADD_LAG and i != 1:
                 grouped = keep.tile([P, PAST], BF16, align_bytes=64, name="early%d" % i)
             else:
                 grouped = work.tile([P, PAST], BF16, align_bytes=64, bufs=6)
@@ -213,15 +201,13 @@ def tile_reverb_prewhiten_replicas_s14_kernel(
         def quant_past(i):
             pc = work.tile([P, GROUPS * P], U32, align_bytes=64)
             ps = work.tile([P, GROUPS * P], U8, align_bytes=64)
-            nc.vector.quantize_mx(out=pc[:].bitcast(FP8X4), scales=ps[:], in_=groupeds[i][:, :PAST])
-            if i in (0, 2):
-                spread_taper(range(1, 4) if i == 0 else range(4, BEAMS), nc.gpsimd.tensor_copy, groupeds[i][:])
+            nc.vector.quantize_mx(out=pc[:].bitcast(FP8X4), scales=ps[:], in_=groupeds[i][:])
             codes_p[i] = (pc, ps)
 
         def predict(i):
             b = i // UNITS
             pc, ps = codes_p.pop(i)
-            pred = psum2.tile([P, NOW], F32)
+            pred = psum4.tile([P, NOW], F32, tag="mx")
             for g in range(GROUPS):
                 nc.tensor.matmul_mx(
                     out=pred[:],
@@ -234,28 +220,33 @@ def tile_reverb_prewhiten_replicas_s14_kernel(
                 )
             preds[i] = pred
 
+        def empty_pred(i):
+            if not vector_subtracts(i):
+                d = work.tile([P, 4, P], F32, align_bytes=64)
+                nc.scalar.copy(out=d[:], in_=preds.pop(i)[:].rearrange("r (p t) -> r t p", t=4))
+                ds[i] = d
+
         def subtract(i):
-            d = work.tile([P, 4, P], F32, align_bytes=64)
-            pred = preds.pop(i)[:].rearrange("r (p t) -> r t p", t=4)
             if vector_subtracts(i):
+                d = work.tile([P, 4, P], F32, align_bytes=64)
                 nc.vector.tensor_tensor(
-                    out=d[:], in0=nows[i // UNITS][:, i % UNITS, :].rearrange("r (p t) -> r t p", t=4), in1=pred,
+                    out=d[:],
+                    in0=preds.pop(i)[:].rearrange("r (p t) -> r t p", t=4),
+                    in1=nows[i // UNITS][:, i % UNITS, :].rearrange("r (p t) -> r t p", t=4),
                     op=ALU.subtract,
                 )
-            else:
-                nc.scalar.activation(out=d[:], in_=pred, func=ACT.Copy, scale=-1.0)
-            ds[i] = d
+                ds[i] = d
 
-        def add_now(i, slots):
+        def take_now(i, slots):
             now_u = nows[i // UNITS][:, i % UNITS, :]
             for t in slots:
-                nc.tensor.matmul(dts[i][:, t, :], lhsT=now_u[:, t::4], rhs=ident16[:], start=(t == 0), stop=(t == 3))
+                nc.tensor.matmul(dts[i][:, t, :], lhsT=now_u[:, t::4], rhs=minus16[:], start=(t == 0), stop=(t == 3))
 
         def turn_now(i):
             dt = psum2.tile([P, 4, P], F32, tag="dt")
             dts[i] = dt
             if not vector_subtracts(i):
-                add_now(i, range(2))
+                take_now(i, range(2))
 
         def turn_d(i):
             d = ds.pop(i)
@@ -265,14 +256,14 @@ def tile_reverb_prewhiten_replicas_s14_kernel(
                     dts[i][:, t, :], lhsT=d[:, t, :], rhs=ident[:], is_transpose=True, start=alone, stop=alone
                 )
             if not alone:
-                add_now(i, range(2, 4))
+                take_now(i, range(2, 4))
 
         def apply_taper(i):
-            e16 = work.tile([P, P, 4], BF16, align_bytes=64)
+            e16 = work.tile([P, NOW], BF16, align_bytes=64)
             nc.vector.tensor_tensor(
-                out=e16[:],
-                in0=tapers[i // UNITS],
-                in1=dts.pop(i)[:].rearrange("p t r -> p r t"),
+                out=e16[:].rearrange("p (a r t) -> p a r t", r=REP, t=4),
+                in0=taper_x[:, i // UNITS].unsqueeze(1).to_broadcast([P, P // REP, REP, 4]),
+                in1=dts.pop(i)[:].rearrange("p t (a r) -> p a r t", r=REP),
                 op=ALU.mult,
             )
             e16s[i] = e16
@@ -280,9 +271,7 @@ def tile_reverb_prewhiten_replicas_s14_kernel(
         def quant_e(i):
             ec = work.tile([P, P], U32, align_bytes=64)
             es = work.tile([P, P], U8, align_bytes=64)
-            nc.vector.quantize_mx(
-                out=ec[:].bitcast(FP8X4), scales=es[:], in_=e16s.pop(i)[:].rearrange("p r t -> p (r t)")
-            )
+            nc.vector.quantize_mx(out=ec[:].bitcast(FP8X4), scales=es[:], in_=e16s.pop(i)[:])
             codes_e[i] = (ec, es)
 
         def pieces(i):
@@ -297,8 +286,8 @@ def tile_reverb_prewhiten_replicas_s14_kernel(
                 y_0 = psum2.tile([P, DOPPLER], F32, tag="turn")
                 y_1 = psum2.tile([P, DOPPLER], F32, tag="turn")
             else:
-                y_0 = psum1.tile([P, DOPPLER], F32)
-                y_1 = psum1.tile([P, DOPPLER], F32)
+                y_0 = psum4.tile([P, DOPPLER], F32, tag="mx")
+                y_1 = psum4.tile([P, DOPPLER], F32, tag="mx")
             if i == STEPS - 1:
                 parts = [(y, slice(256 * h, 256 * (h + 1)), DOPPLER * h + 256 * k) for k, y in enumerate((y_0, y_1)) for h in range(2)]
             else:
@@ -318,8 +307,7 @@ def tile_reverb_prewhiten_replicas_s14_kernel(
 
         def square(i):
             sq = work.tile([P, 2, DOPPLER], F32, align_bytes=64)
-            y_0, y_1 = ys.pop(i)
-            for h, y in enumerate((y_0, y_1)):
+            for h, y in enumerate(ys.pop(i)):
                 nc.scalar.activation(out=sq[:, h, :], in_=y[:], func=ACT.Square)
             sqs[i] = sq
 
@@ -351,62 +339,43 @@ def tile_reverb_prewhiten_replicas_s14_kernel(
                 )
 
         def helps(i):
-            if 2 < i < ADD_LAG:
-                help_widen(0, 2, groupeds.pop(i)[:])
-            elif i >= ADD_LAG and vector_subtracts(i - 1):
-                help_widen(i + 5, 1)
+            if i < ADD_LAG:
+                first = min(j for j in range(STEPS) if early_for_gpsimd(j) and cast[j] == 0)
+                widen(nc.gpsimd.tensor_copy, first, PAST, groupeds.pop(i)[:])
+            elif vector_subtracts(i - 1):
+                for j in [j for j in range(i + 5, STEPS) if cast[j] < PAST][:1]:
+                    widen(nc.gpsimd.tensor_copy, j, LONG_CAST)
 
-        def casts(i):
-            s = i - 7
-            if s < -3:
-                widen_upto(min(i + 1 + i // 2, UNITS))
-            else:
-                even = LEAD + (STEPS - LEAD) * s // (STEPS - 8)
-                widen_upto(max(i + 1, min(FILL_CASTS * (s + 5), even)))
+        def casts(s):
+            widen_upto(max(s + 8, LEAD + (STEPS - LEAD) * s // CAST_STEPS))
 
-        for s in range(-7, STEPS + 3):
-            plan = (
-                (apply_taper, s),
-                (quant_past, s + 3),
-                (quant_e, s),
-                (add, s - 2),
-                (helps, s + 3),
-                (scale_past, s + 4),
-                (subtract, s + 2),
-                (correlate, s),
-                (predict, s + 3),
-                (square, s),
-                (root, s - 2),
-                (casts, s + 7),
-                (turn_now, s + 2),
-                (turn_past, s + 6),
-                (turn_d, s + 2),
-            )
-            if s + 3 >= STEPS:
-                plan = (
-                    (apply_taper, s),
-                    (add, s - 2),
-                    (quant_e, s),
-                    (subtract, s + 2),
-                    (correlate, s),
-                    (root, s - 2),
-                    (square, s),
-                    (turn_now, s + 2),
-                    (turn_d, s + 2),
-                )
-            if s == -3:
-                plan = ((quant_past, 0), (scale_past, 1), (helps, 0), (predict, 0), (casts, 4), (turn_past, 3))
-            if s == -2:
-                plan = tuple(step for step in plan if step[0] not in (quant_past, predict))
-            if s == -1:
-                plan = ((quant_past, 1), (predict, 1)) + plan
-            if s == -6:
-                help_widen(UNITS - 1, 2)
-            if s == -4:
-                turn_taper()
-                spread_taper(range(1), nc.scalar.copy, taper_0[:])
+        def run(*plan):
             for stage, i in plan:
                 if 0 <= i < STEPS:
                     stage(i)
+
+        widen_upto(3)
+        widen(nc.gpsimd.tensor_copy, 3, PAST)
+        run((turn_past, 0), (turn_past, 1))
+        widen_upto(6)
+        turn_taper()
+        widen_upto(7)
+        spread_taper()
+        run((scale_past, 0), (turn_past, 2), (quant_past, 0), (helps, 0), (scale_past, 1), (predict, 0))
+        widen_upto(H1)
+        run((turn_past, 3), (scale_past, 2), (empty_pred, 0))
+        widen_upto(H2)
+        run((turn_now, 0), (turn_past, 4), (turn_d, 0))
+        run((quant_past, 1), (quant_past, 2), (helps, 2), (predict, 1), (predict, 2), (scale_past, 3), (empty_pred, 1))
+        widen_upto(H3)
+        run((empty_pred, 2), (turn_now, 1), (turn_past, 5), (turn_d, 1))
+        for s in range(STEPS + 2):
+            if s + 3 < STEPS:
+                run((apply_taper, s), (quant_past, s + 3), (quant_e, s), (add, s - 2), (helps, s + 3), (scale_past, s + 4))
+                run((subtract, s + 2), (correlate, s), (predict, s + 3), (square, s), (empty_pred, s + 3), (root, s - 2))
+                casts(s)
+            else:
+                run((apply_taper, s), (add, s - 2), (quant_e, s), (subtract, s + 2), (correlate, s), (root, s - 2), (square, s))
+            run((turn_now, s + 2), (turn_past, s + 6), (turn_d, s + 2))
             if s >= UNITS and s % UNITS == 0 and s // UNITS + HELD - 1 < BEAMS:
                 load_beam(s // UNITS + HELD - 1)

@@ -13,12 +13,15 @@ GROUPS = PAST // 512
 ADD_LAG = 5
 HELD = 4
 TAIL = 2
-EVERY = 5
-LONG_CAST = 640
-LEAD = 20
-CAST_STEPS = 22
-RAWS = 16
-H1, H2, H3 = 9, 14, 18
+EVERY, FIRST = 7, 5
+SET = 5
+PIECE = SET * DOPPLER // (SET - 1)
+PIECED = 25
+LONG_CAST = 384
+LATE = 23
+BEFORE_COPY = (9, 14, 18)
+RAWS = 13
+GROUPEDS = 9
 REP = 8
 
 F32 = mybir.dt.float32
@@ -146,10 +149,10 @@ def tile_reverb_prewhiten_replicas_s14_kernel(
         raws, turned, groupeds, codes_p, preds, ds, dts, e16s, codes_e, ys, sqs, sums = ({} for k in range(12))
 
         def vector_subtracts(i):
-            return (i % EVERY == EVERY - 1 and i < STEPS - ADD_LAG) or i >= STEPS - TAIL
+            return i % EVERY == FIRST or i >= STEPS - TAIL
 
-        def early_for_gpsimd(i):
-            return i % UNITS == UNITS - 1 and i < LEAD
+        def for_gpsimd(i):
+            return i % UNITS == UNITS - 1 or (i >= LATE and i % 2 == 1)
 
         def spans(i):
             return [range(g, g + 1) for g in range(GROUPS)] if i == 0 else [range(GROUPS)]
@@ -166,7 +169,7 @@ def tile_reverb_prewhiten_replicas_s14_kernel(
 
         def widen_upto(units):
             for i in range(min(units, STEPS)):
-                while cast[i] < PAST and not early_for_gpsimd(i):
+                while cast[i] < PAST and not for_gpsimd(i):
                     widen(nc.scalar.copy, i, 512 if i == 0 else PAST)
 
         def turn_past(i):
@@ -188,7 +191,7 @@ def tile_reverb_prewhiten_replicas_s14_kernel(
             if i < ADD_LAG and i != 1:
                 grouped = keep.tile([P, PAST], BF16, align_bytes=64, name="early%d" % i)
             else:
-                grouped = work.tile([P, PAST], BF16, align_bytes=64, bufs=6)
+                grouped = work.tile([P, 2 * PIECE], BF16, align_bytes=64, bufs=GROUPEDS)
             for groups, tp in zip(spans(i), turned.pop(i)):
                 nc.vector.tensor_tensor(
                     out=grouped[:, 512 * groups.start : 512 * groups.stop].rearrange("p (q u e) -> p q u e", u=2, e=2),
@@ -201,7 +204,7 @@ def tile_reverb_prewhiten_replicas_s14_kernel(
         def quant_past(i):
             pc = work.tile([P, GROUPS * P], U32, align_bytes=64)
             ps = work.tile([P, GROUPS * P], U8, align_bytes=64)
-            nc.vector.quantize_mx(out=pc[:].bitcast(FP8X4), scales=ps[:], in_=groupeds[i][:])
+            nc.vector.quantize_mx(out=pc[:].bitcast(FP8X4), scales=ps[:], in_=groupeds[i][:, :PAST])
             codes_p[i] = (pc, ps)
 
         def predict(i):
@@ -242,11 +245,15 @@ def tile_reverb_prewhiten_replicas_s14_kernel(
             for t in slots:
                 nc.tensor.matmul(dts[i][:, t, :], lhsT=now_u[:, t::4], rhs=minus16[:], start=(t == 0), stop=(t == 3))
 
+        def lent(i):
+            return 0 < i < STEPS and vector_subtracts(i - 1) and not vector_subtracts(i)
+
         def turn_now(i):
-            dt = psum2.tile([P, 4, P], F32, tag="dt")
-            dts[i] = dt
+            if not lent(i):
+                dt = psum2.tile([P, 4, P], F32, tag="dt")
+                dts[i] = dt
             if not vector_subtracts(i):
-                take_now(i, range(2))
+                take_now(i, range(1 if lent(i) else 0, 2))
 
         def turn_d(i):
             d = ds.pop(i)
@@ -257,6 +264,12 @@ def tile_reverb_prewhiten_replicas_s14_kernel(
                 )
             if not alone:
                 take_now(i, range(2, 4))
+
+        def lend(i):
+            if lent(i):
+                dt = psum2.tile([P, 4, P], F32, tag="dt")
+                dts[i] = dt
+                take_now(i, range(1))
 
         def apply_taper(i):
             e16 = work.tile([P, NOW], BF16, align_bytes=64)
@@ -306,18 +319,33 @@ def tile_reverb_prewhiten_replicas_s14_kernel(
             ys[i] = (y_0, y_1)
 
         def square(i):
-            sq = work.tile([P, 2, DOPPLER], F32, align_bytes=64)
+            if i >= PIECED:
+                sq = work.tile([P, 2, DOPPLER], F32, align_bytes=64, bufs=3)
+                sqs[i] = sq
+                home = sq[:]
+            else:
+                if i % SET == 0:
+                    sq_set = work.tile([P, 2, SET * DOPPLER], F32, align_bytes=64, bufs=2)
+                    sqs["set", i // SET] = sq_set
+                home = sqs["set", i // SET][:, :, DOPPLER * (i % SET) : DOPPLER * (i % SET + 1)]
             for h, y in enumerate(ys.pop(i)):
-                nc.scalar.activation(out=sq[:, h, :], in_=y[:], func=ACT.Square)
-            sqs[i] = sq
+                nc.scalar.activation(out=home[:, h, :], in_=y[:], func=ACT.Square)
 
         def add(i):
+            if i < PIECED:
+                if i % SET:
+                    cols = slice(PIECE * (i % SET - 1), PIECE * (i % SET))
+                    sq = sqs["set", i // SET]
+                    power = groupeds.pop(i + ADD_LAG)[:].bitcast(F32)
+                    nc.gpsimd.tensor_tensor(out=power, in0=sq[:, 0, cols], in1=sq[:, 1, cols], op=ALU.add)
+                    sums[i] = power
+                return
             sq = sqs.pop(i)
             if i + ADD_LAG < STEPS:
-                power = groupeds.pop(i + ADD_LAG)[:].bitcast(F32)
+                power = groupeds.pop(i + ADD_LAG)[:, :PAST].bitcast(F32)
                 nc.gpsimd.tensor_tensor(out=power, in0=sq[:, 0, :], in1=sq[:, 1, :], op=ALU.add)
             else:
-                total = work.tile([P, DOPPLER], F32, align_bytes=64)
+                total = work.tile([P, DOPPLER], F32, align_bytes=64, bufs=3)
                 power = total[:]
                 if i == STEPS - 1:
                     for k in range(2):
@@ -328,26 +356,44 @@ def tile_reverb_prewhiten_replicas_s14_kernel(
                     nc.vector.tensor_tensor(out=power, in0=sq[:, 0, :], in1=sq[:, 1, :], op=ALU.add)
             sums[i] = power
 
+        def store(queue, first, env):
+            row = UNITS * DOPPLER
+            last = first + env.shape[1]
+            for b in range(first // row, (last - 1) // row + 1):
+                lo, hi = max(first, row * b), min(last, row * (b + 1))
+                queue.dma_start(
+                    out=out[b].rearrange("(r j) d -> r (j d)", j=UNITS)[:, lo - row * b : hi - row * b],
+                    in_=env[:, lo - first : hi - first],
+                )
+
         def root(i):
-            env = outs.tile([P, DOPPLER], F32, align_bytes=64)
+            if i not in sums:
+                return
+            env = outs.tile([P, PIECE], F32, align_bytes=64, bufs=6)
             power = sums.pop(i)
+            if i < PIECED:
+                nc.scalar.activation(out=env[:], in_=power, func=ACT.Sqrt)
+                store(nc.sync, SET * DOPPLER * (i // SET) + PIECE * (i % SET - 1), env[:])
+                return
             for cols in pieces(i):
                 nc.scalar.activation(out=env[:, cols], in_=power[:, cols], func=ACT.Sqrt)
                 queue = nc.scalar if i == STEPS - 1 and cols.stop == DOPPLER else nc.sync
-                queue.dma_start(
-                    out=out[i // UNITS].rearrange("(r j) d -> r j d", j=UNITS)[:, i % UNITS, cols], in_=env[:, cols]
-                )
+                store(queue, DOPPLER * i + cols.start, env[:, cols])
 
         def helps(i):
-            if i < ADD_LAG:
-                first = min(j for j in range(STEPS) if early_for_gpsimd(j) and cast[j] == 0)
-                widen(nc.gpsimd.tensor_copy, first, PAST, groupeds.pop(i)[:])
-            elif vector_subtracts(i - 1):
-                for j in [j for j in range(i + 5, STEPS) if cast[j] < PAST][:1]:
+            if i in groupeds:
+                home = groupeds.pop(i)[:, :PAST]
+                for j in [j for j in range(STEPS) if for_gpsimd(j) and cast[j] == 0][:1]:
+                    widen(nc.gpsimd.tensor_copy, j, PAST, home)
+            if vector_subtracts(i - 1):
+                for j in [j for j in range(i + 5, STEPS) if cast[j] < PAST and not for_gpsimd(j)][:1]:
                     widen(nc.gpsimd.tensor_copy, j, LONG_CAST)
 
         def casts(s):
-            widen_upto(max(s + 8, LEAD + (STEPS - LEAD) * s // CAST_STEPS))
+            widen_upto(s + 8)
+            if s < UNITS or (s - 2) % SET == 0:
+                for j in [j for j in range(STEPS) if cast[j] < PAST and not for_gpsimd(j)][:1]:
+                    widen_upto(j + 1)
 
         def run(*plan):
             for stage, i in plan:
@@ -362,16 +408,16 @@ def tile_reverb_prewhiten_replicas_s14_kernel(
         widen_upto(7)
         spread_taper()
         run((scale_past, 0), (turn_past, 2), (quant_past, 0), (helps, 0), (scale_past, 1), (predict, 0))
-        widen_upto(H1)
+        widen_upto(BEFORE_COPY[0])
         run((turn_past, 3), (scale_past, 2), (empty_pred, 0))
-        widen_upto(H2)
-        run((turn_now, 0), (turn_past, 4), (turn_d, 0))
+        widen_upto(BEFORE_COPY[1])
+        run((turn_past, 4), (turn_now, 0), (turn_d, 0))
         run((quant_past, 1), (quant_past, 2), (helps, 2), (predict, 1), (predict, 2), (scale_past, 3), (empty_pred, 1))
-        widen_upto(H3)
+        widen_upto(BEFORE_COPY[2])
         run((empty_pred, 2), (turn_now, 1), (turn_past, 5), (turn_d, 1))
         for s in range(STEPS + 2):
             if s + 3 < STEPS:
-                run((apply_taper, s), (quant_past, s + 3), (quant_e, s), (add, s - 2), (helps, s + 3), (scale_past, s + 4))
+                run((apply_taper, s), (lend, s + 2), (quant_past, s + 3), (quant_e, s), (add, s - 2), (helps, s + 3), (scale_past, s + 4))
                 run((subtract, s + 2), (correlate, s), (predict, s + 3), (square, s), (empty_pred, s + 3), (root, s - 2))
                 casts(s)
             else:

@@ -13,11 +13,13 @@ GROUPS = PAST // 512
 ADD_LAG = 5
 HELD = 4
 TAIL = 2
-EVERY, FIRST = 7, 5
 SET = 5
-PIECE = SET * DOPPLER // (SET - 1)
-PIECED = 25
-LONG_CAST = 384
+CUTS = (0, 576, 1152, 1984, 2560)
+LAST_SET = 20
+GPSIMD_SUMS = 27
+RING = 2 * SET
+WIDEST = 832
+EARLY = 3
 LATE = 23
 BEFORE_COPY = (9, 14, 18)
 RAWS = 13
@@ -56,6 +58,7 @@ def tile_reverb_prewhiten_replicas_s14_kernel(
         taper_rows = keep.tile([P, NOW], BF16, align_bytes=64)
         taper_x = keep.tile([P, BEAMS, REP, 4], BF16, align_bytes=64)
         ident = keep.tile([P, P], F32, align_bytes=64)
+        sq_ring = keep.tile([P, 2, RING * DOPPLER], F32, align_bytes=64)
         minus16 = keep.tile([P, P], BF16, align_bytes=64)
 
         pasts, nows, coefs, banks = {}, {}, {}, {}
@@ -70,12 +73,12 @@ def tile_reverb_prewhiten_replicas_s14_kernel(
                 nc.sync.dma_start(out=pasts[b][:, units, cols], in_=src[:, units, cols])
 
         def load_now(b):
-            now_sb = inp.tile([P, UNITS, NOW], BF16, align_bytes=64, bufs=HELD + 1)
+            now_sb = inp.tile([P, UNITS, NOW], BF16, align_bytes=64, bufs=HELD)
             nc.sync.dma_start(out=now_sb[:], in_=now[b].rearrange("(r j) n -> r j n", j=UNITS))
             nows[b] = now_sb
 
         def load_coef(b):
-            coef = inp.tile([P, GROUPS, 2 * NOW], U8, align_bytes=64, bufs=HELD + 1)
+            coef = inp.tile([P, GROUPS, 2 * NOW], U8, align_bytes=64, bufs=HELD)
             groups = slice(GROUPS * b, GROUPS * (b + 1))
             nc.sync.dma_start(out=coef[:].bitcast(I32), in_=coef_words[groups].rearrange("g p n -> p g n").bitcast(I32))
             coefs[b] = coef
@@ -89,7 +92,7 @@ def tile_reverb_prewhiten_replicas_s14_kernel(
                 )
 
         def load_bank(b):
-            bank = inp.tile([P, 4 * DOPPLER], U8, align_bytes=64, bufs=HELD + 1)
+            bank = inp.tile([P, 4 * DOPPLER], U8, align_bytes=64, bufs=HELD)
             nc.sync.dma_start(out=bank[:].bitcast(I32), in_=bank_words[b].bitcast(I32))
             for r in range(4):
                 nc.sync.dma_start(out=bank_s[b][r:P:32, :].bitcast(I32), in_=bank_scales[b, r:16:4, :].bitcast(I32))
@@ -146,10 +149,10 @@ def tile_reverb_prewhiten_replicas_s14_kernel(
             nc.scalar.copy(out=words[:, :, 1:, :], in_=words[:, :, 0:1, :].to_broadcast([P, BEAMS, REP - 1, 2]))
 
         cast = [0] * STEPS
-        raws, turned, groupeds, codes_p, preds, ds, dts, e16s, codes_e, ys, sqs, sums = ({} for k in range(12))
+        raws, turned, groupeds, codes_p, preds, ds, dts, e16s, codes_e, ys, sums = ({} for k in range(11))
 
         def vector_subtracts(i):
-            return i % EVERY == FIRST or i >= STEPS - TAIL
+            return (i % SET == 2 and i < LAST_SET + SET) or i >= STEPS - TAIL
 
         def for_gpsimd(i):
             return i % UNITS == UNITS - 1 or (i >= LATE and i % 2 == 1)
@@ -191,7 +194,7 @@ def tile_reverb_prewhiten_replicas_s14_kernel(
             if i < ADD_LAG and i != 1:
                 grouped = keep.tile([P, PAST], BF16, align_bytes=64, name="early%d" % i)
             else:
-                grouped = work.tile([P, 2 * PIECE], BF16, align_bytes=64, bufs=GROUPEDS)
+                grouped = work.tile([P, 2 * WIDEST], BF16, align_bytes=64, bufs=GROUPEDS)
             for groups, tp in zip(spans(i), turned.pop(i)):
                 nc.vector.tensor_tensor(
                     out=grouped[:, 512 * groups.start : 512 * groups.stop].rearrange("p (q u e) -> p q u e", u=2, e=2),
@@ -204,7 +207,13 @@ def tile_reverb_prewhiten_replicas_s14_kernel(
         def quant_past(i):
             pc = work.tile([P, GROUPS * P], U32, align_bytes=64)
             ps = work.tile([P, GROUPS * P], U8, align_bytes=64)
-            nc.vector.quantize_mx(out=pc[:].bitcast(FP8X4), scales=ps[:], in_=groupeds[i][:, :PAST])
+            for groups in spans(i):
+                words = slice(P * groups.start, P * groups.stop)
+                nc.vector.quantize_mx(
+                    out=pc[:, words].bitcast(FP8X4),
+                    scales=ps[:, words],
+                    in_=groupeds[i][:, 4 * words.start : 4 * words.stop],
+                )
             codes_p[i] = (pc, ps)
 
         def predict(i):
@@ -272,7 +281,12 @@ def tile_reverb_prewhiten_replicas_s14_kernel(
                 take_now(i, range(1))
 
         def apply_taper(i):
-            e16 = work.tile([P, NOW], BF16, align_bytes=64)
+            if i + ADD_LAG - 2 < STEPS:
+                e16 = work.tile([P, NOW], BF16, align_bytes=64)
+            else:
+                grouped = work.tile([P, 2 * WIDEST], BF16, align_bytes=64, bufs=GROUPEDS)
+                groupeds[i + ADD_LAG - 2] = grouped
+                e16 = grouped[:, :NOW]
             nc.vector.tensor_tensor(
                 out=e16[:].rearrange("p (a r t) -> p a r t", r=REP, t=4),
                 in0=taper_x[:, i // UNITS].unsqueeze(1).to_broadcast([P, P // REP, REP, 4]),
@@ -287,10 +301,10 @@ def tile_reverb_prewhiten_replicas_s14_kernel(
             nc.vector.quantize_mx(out=ec[:].bitcast(FP8X4), scales=es[:], in_=e16s.pop(i)[:])
             codes_e[i] = (ec, es)
 
-        def pieces(i):
+        def pieces(i, width):
             if i == STEPS - 1:
                 return (slice(0, DOPPLER // 2), slice(DOPPLER // 2, DOPPLER))
-            return (slice(0, DOPPLER),)
+            return (slice(0, width),)
 
         def correlate(i):
             b = i // UNITS
@@ -318,43 +332,48 @@ def tile_reverb_prewhiten_replicas_s14_kernel(
                 )
             ys[i] = (y_0, y_1)
 
+        def piece(i):
+            if i >= GPSIMD_SUMS:
+                return range(DOPPLER * i, DOPPLER * (i + 1))
+            first = DOPPLER * SET * min(i // SET, LAST_SET // SET)
+            if i < LAST_SET:
+                return range(first + CUTS[max(i % SET - 1, 0)], first + CUTS[i % SET])
+            count = GPSIMD_SUMS - LAST_SET
+            ends = [DOPPLER * count * k // (count - 1) // 16 * 16 for k in range(count)]
+            return range(first + ends[max(i - LAST_SET - 1, 0)], first + ends[i - LAST_SET])
+
+        def squares(cols):
+            first = cols.start % (RING * DOPPLER)
+            return sq_ring[:, :, first : first + len(cols)]
+
         def square(i):
-            if i >= PIECED:
-                sq = work.tile([P, 2, DOPPLER], F32, align_bytes=64, bufs=3)
-                sqs[i] = sq
-                home = sq[:]
-            else:
-                if i % SET == 0:
-                    sq_set = work.tile([P, 2, SET * DOPPLER], F32, align_bytes=64, bufs=2)
-                    sqs["set", i // SET] = sq_set
-                home = sqs["set", i // SET][:, :, DOPPLER * (i % SET) : DOPPLER * (i % SET + 1)]
-            for h, y in enumerate(ys.pop(i)):
-                nc.scalar.activation(out=home[:, h, :], in_=y[:], func=ACT.Square)
+            home = squares(range(DOPPLER * i, DOPPLER * (i + 1)))
+            for h in range(1 if i == STEPS - 2 else 2):
+                nc.scalar.activation(out=home[:, h, :], in_=ys[i][h][:], func=ACT.Square)
+
+        def square_on_vector(i):
+            held = keep.tile([P, DOPPLER], F32, align_bytes=64)
+            nc.vector.tensor_copy(out=held[:], in_=ys[i][1][:])
+            nc.vector.tensor_tensor(out=squares(piece(i))[:, 1, :], in0=ys[i][1][:], in1=held[:], op=ALU.mult)
 
         def add(i):
-            if i < PIECED:
-                if i % SET:
-                    cols = slice(PIECE * (i % SET - 1), PIECE * (i % SET))
-                    sq = sqs["set", i // SET]
-                    power = groupeds.pop(i + ADD_LAG)[:].bitcast(F32)
-                    nc.gpsimd.tensor_tensor(out=power, in0=sq[:, 0, cols], in1=sq[:, 1, cols], op=ALU.add)
-                    sums[i] = power
-                return
-            sq = sqs.pop(i)
-            if i + ADD_LAG < STEPS:
-                power = groupeds.pop(i + ADD_LAG)[:, :PAST].bitcast(F32)
+            if piece(i):
+                sq = squares(piece(i))
+                power = groupeds.pop(i + ADD_LAG)[:].bitcast(F32)[:, : sq.shape[2]]
                 nc.gpsimd.tensor_tensor(out=power, in0=sq[:, 0, :], in1=sq[:, 1, :], op=ALU.add)
+                sums[i] = power
+
+        def add_on_vector(i):
+            sq = squares(piece(i))
+            total = work.tile([P, DOPPLER], F32, align_bytes=64, bufs=3)
+            if i == STEPS - 1:
+                for k in range(2):
+                    nc.vector.tensor_tensor(
+                        out=total[:, 256 * k : 256 * (k + 1)], in0=sq[:, k, :256], in1=sq[:, k, 256:], op=ALU.add
+                    )
             else:
-                total = work.tile([P, DOPPLER], F32, align_bytes=64, bufs=3)
-                power = total[:]
-                if i == STEPS - 1:
-                    for k in range(2):
-                        nc.vector.tensor_tensor(
-                            out=power[:, 256 * k : 256 * (k + 1)], in0=sq[:, k, :256], in1=sq[:, k, 256:], op=ALU.add
-                        )
-                else:
-                    nc.vector.tensor_tensor(out=power, in0=sq[:, 0, :], in1=sq[:, 1, :], op=ALU.add)
-            sums[i] = power
+                nc.vector.tensor_tensor(out=total[:], in0=sq[:, 0, :], in1=sq[:, 1, :], op=ALU.add)
+            sums[i] = total[:]
 
         def store(queue, first, env):
             row = UNITS * DOPPLER
@@ -367,31 +386,23 @@ def tile_reverb_prewhiten_replicas_s14_kernel(
                 )
 
         def root(i):
-            if i not in sums:
-                return
-            env = outs.tile([P, PIECE], F32, align_bytes=64, bufs=6)
-            power = sums.pop(i)
-            if i < PIECED:
-                nc.scalar.activation(out=env[:], in_=power, func=ACT.Sqrt)
-                store(nc.sync, SET * DOPPLER * (i // SET) + PIECE * (i % SET - 1), env[:])
-                return
-            for cols in pieces(i):
-                nc.scalar.activation(out=env[:, cols], in_=power[:, cols], func=ACT.Sqrt)
-                queue = nc.scalar if i == STEPS - 1 and cols.stop == DOPPLER else nc.sync
-                store(queue, DOPPLER * i + cols.start, env[:, cols])
+            if i in sums:
+                env = outs.tile([P, WIDEST], F32, align_bytes=64, bufs=5)
+                power = sums.pop(i)
+                for cols in pieces(i, power.shape[1]):
+                    nc.scalar.activation(out=env[:, cols], in_=power[:, cols], func=ACT.Sqrt)
+                    queue = nc.scalar if i == STEPS - 1 and cols.stop == DOPPLER else nc.sync
+                    store(queue, piece(i).start + cols.start, env[:, cols])
 
         def helps(i):
             if i in groupeds:
                 home = groupeds.pop(i)[:, :PAST]
                 for j in [j for j in range(STEPS) if for_gpsimd(j) and cast[j] == 0][:1]:
                     widen(nc.gpsimd.tensor_copy, j, PAST, home)
-            if vector_subtracts(i - 1):
-                for j in [j for j in range(i + 5, STEPS) if cast[j] < PAST and not for_gpsimd(j)][:1]:
-                    widen(nc.gpsimd.tensor_copy, j, LONG_CAST)
 
         def casts(s):
             widen_upto(s + 8)
-            if s < UNITS or (s - 2) % SET == 0:
+            if s < EARLY or not piece(s - 2) or vector_subtracts(s + 3):
                 for j in [j for j in range(STEPS) if cast[j] < PAST and not for_gpsimd(j)][:1]:
                     widen_upto(j + 1)
 
@@ -415,13 +426,16 @@ def tile_reverb_prewhiten_replicas_s14_kernel(
         run((quant_past, 1), (quant_past, 2), (helps, 2), (predict, 1), (predict, 2), (scale_past, 3), (empty_pred, 1))
         widen_upto(BEFORE_COPY[2])
         run((empty_pred, 2), (turn_now, 1), (turn_past, 5), (turn_d, 1))
-        for s in range(STEPS + 2):
-            if s + 3 < STEPS:
-                run((apply_taper, s), (lend, s + 2), (quant_past, s + 3), (quant_e, s), (add, s - 2), (helps, s + 3), (scale_past, s + 4))
-                run((subtract, s + 2), (correlate, s), (predict, s + 3), (square, s), (empty_pred, s + 3), (root, s - 2))
-                casts(s)
-            else:
-                run((apply_taper, s), (add, s - 2), (quant_e, s), (subtract, s + 2), (correlate, s), (root, s - 2), (square, s))
+        for s in range(STEPS - 3):
+            run((apply_taper, s), (lend, s + 2), (quant_past, s + 3), (quant_e, s), (add, s - 2), (helps, s + 3), (scale_past, s + 4))
+            run((subtract, s + 2), (correlate, s), (predict, s + 3), (square, s), (empty_pred, s + 3), (root, s - 2))
+            casts(s)
             run((turn_now, s + 2), (turn_past, s + 6), (turn_d, s + 2))
             if s >= UNITS and s % UNITS == 0 and s // UNITS + HELD - 1 < BEAMS:
                 load_beam(s // UNITS + HELD - 1)
+        a, b, c = range(STEPS - 3, STEPS)
+        run((apply_taper, a), (quant_e, a), (add, a - 2), (subtract, c), (correlate, a), (turn_now, c), (turn_d, c))
+        run((square, a), (root, a - 2), (apply_taper, b), (quant_e, b), (correlate, b), (square, b))
+        run((apply_taper, c), (add_on_vector, a - 1), (quant_e, c), (correlate, c), (root, a - 1))
+        run((add, a), (square_on_vector, b), (square, c), (root, a), (add_on_vector, b), (root, b))
+        run((add_on_vector, c), (root, c))

@@ -402,7 +402,7 @@ def tile_reverb_prewhiten_replicas_s14_kernel(
 
         def casts(s):
             widen_upto(s + 8)
-            if s < EARLY or not piece(s - 2) or vector_subtracts(s + 3):
+            if s < EARLY or vector_subtracts(s + 3) or (s > STEPS // 2 and not piece(s - 2)):
                 for j in [j for j in range(STEPS) if cast[j] < PAST and not for_gpsimd(j)][:1]:
                     widen_upto(j + 1)
 

@@ -242,9 +242,9 @@ def tile_reverb_prewhiten_replicas_s14_kernel(
             if vector_subtracts(i):
                 d = work.tile([P, 4, P], F32, align_bytes=64)
                 nc.vector.tensor_tensor(
-                    out=d[:],
-                    in0=preds.pop(i)[:].rearrange("r (p t) -> r t p", t=4),
-                    in1=nows[i // UNITS][:, i % UNITS, :].rearrange("r (p t) -> r t p", t=4),
+                    out=d[:].rearrange("r (h e) p -> r h p e", h=2),
+                    in0=preds.pop(i)[:].rearrange("r (p h e) -> r h p e", h=2, e=2),
+                    in1=nows[i // UNITS][:, i % UNITS, :].rearrange("r (p h e) -> r h p e", h=2, e=2),
                     op=ALU.subtract,
                 )
                 ds[i] = d

@@ -45,10 +45,7 @@ def tile_reverb_prewhiten_replicas_s14_kernel(
     with ExitStack() as ctx:
         keep = ctx.enter_context(tc.tile_pool(name="keep", bufs=1))
         inp = ctx.enter_context(tc.tile_pool(name="inp", bufs=BEAMS))
-        work = ctx.enter_context(tc.tile_pool(name="work", bufs=4))
-        outs = ctx.enter_context(tc.tile_pool(name="outs", bufs=8))
-        psum2 = ctx.enter_context(tc.psum_pool(name="psum2", bufs=2))
-        psum4 = ctx.enter_context(tc.psum_pool(name="psum4", bufs=4))
+        psum = ctx.enter_context(tc.psum_pool(name="psum", bufs=1))
         ctx.enter_context(tc.manual_schedule())
 
         coef_s = [keep.tile([P, GROUPS * NOW], U8, align_bytes=64, name="coef_s%d" % b) for b in range(HELD)] * 2
@@ -60,6 +57,33 @@ def tile_reverb_prewhiten_replicas_s14_kernel(
         ident = keep.tile([P, P], F32, align_bytes=64)
         sq_ring = keep.tile([P, 2, RING * DOPPLER], F32, align_bytes=64)
         minus16 = keep.tile([P, P], BF16, align_bytes=64)
+
+        def ring(pool, name, count, width, dtype):
+            if pool is psum:
+                return [pool.tile([P, width], dtype, name="%s%d" % (name, k))[:] for k in range(count)]
+            return [pool.tile([P, width], dtype, align_bytes=64, name="%s%d" % (name, k))[:] for k in range(count)]
+
+        free_turn, free_dt, free_mx = (ring(psum, n, c, 512, F32) for n, c in (("turn", 2), ("dt", 2), ("mx", 4)))
+        free_raw = ring(keep, "raw", RAWS, PAST, BF16)
+        free_grouped = ring(keep, "grouped", GROUPEDS, 2 * WIDEST, BF16)
+        ring_pc, ring_ps = ring(keep, "pc", 4, GROUPS * P, U32), ring(keep, "ps", 4, GROUPS * P, U8)
+        ring_ec, ring_es = ring(keep, "ec", 4, P, U32), ring(keep, "es", 4, P, U8)
+        ring_d, ring_e = ring(keep, "d", 4, NOW, F32), ring(keep, "e", 4, NOW, BF16)
+        ring_env, ring_total = ring(keep, "env", 5, WIDEST, F32), ring(keep, "total", 3, DOPPLER, F32)
+        homes = {}
+
+        def turn(tiles):
+            tiles.append(tiles.pop(0))
+            return tiles[-1]
+
+        def take(free, key):
+            homes[key] = (free, free.pop(0))
+            return homes[key][1]
+
+        def give(key):
+            if key in homes:
+                free, tile = homes.pop(key)
+                free.append(tile)
 
         pasts, nows, coefs, banks = {}, {}, {}, {}
         whole = [(slice(0, UNITS), slice(0, PAST))]
@@ -133,7 +157,7 @@ def tile_reverb_prewhiten_replicas_s14_kernel(
             nc.vector.tensor_copy(out=scale_x[:, g], in_=scale_sb[:, g : g + 1, :].to_broadcast([P, P, 4]))
 
         def turn_taper():
-            tp = psum2.tile([P, 2, P], F32, tag="dt")
+            tp = take(free_dt, "taper")[:, : 2 * P].rearrange("p (u r) -> p u r", u=2)
             words = taper_rows[:].bitcast(F32)
             for u in range(2):
                 nc.tensor.transpose(tp[:, u, :], words[:, u::2], ident[:])
@@ -143,6 +167,7 @@ def tile_reverb_prewhiten_replicas_s14_kernel(
                 func=ACT.Copy,
                 scale=-1.0,
             )
+            give("taper")
 
         def spread_taper():
             words = taper_x[:].bitcast(F32)
@@ -163,8 +188,7 @@ def tile_reverb_prewhiten_replicas_s14_kernel(
         def widen(copy, i, count, home=None):
             if i not in raws:
                 if home is None:
-                    raw = work.tile([P, PAST], BF16, align_bytes=64, bufs=RAWS)
-                    home = raw[:]
+                    home = take(free_raw, ("raw", i))
                 raws[i] = home
             cols = slice(cast[i], min(cast[i] + count, PAST))
             copy(out=raws[i][:, cols], in_=pasts[i // UNITS][:, i % UNITS, cols].bitcast(FP8))
@@ -179,22 +203,21 @@ def tile_reverb_prewhiten_replicas_s14_kernel(
             words = raws.pop(i).bitcast(F32)
             turned[i] = []
             for groups in spans(i):
-                if i == 3 or groups.start > 0:
-                    tp = psum4.tile([P, 2, len(groups) * P], F32, tag="mx")
-                else:
-                    tp = psum2.tile([P, 2, len(groups) * P], F32, tag="turn")
+                bank = take(free_mx if i == 3 or groups.start > 0 else free_turn, ("turned", i, groups.start))
+                tp = bank[:, : 2 * len(groups) * P].rearrange("p (u r) -> p u r", u=2)
                 for n, g in enumerate(groups):
                     for u in range(2):
                         nc.tensor.transpose(
                             tp[:, u, P * n : P * (n + 1)], words[:, 256 * g + u : 256 * (g + 1) : 2], ident[:]
                         )
                 turned[i].append(tp)
+            give(("raw", i))
 
         def scale_past(i):
             if i < ADD_LAG and i != 1:
-                grouped = keep.tile([P, PAST], BF16, align_bytes=64, name="early%d" % i)
+                grouped = keep.tile([P, PAST], BF16, align_bytes=64, name="early%d" % i)[:]
             else:
-                grouped = work.tile([P, 2 * WIDEST], BF16, align_bytes=64, bufs=GROUPEDS)
+                grouped = take(free_grouped, ("grouped", i))
             for groups, tp in zip(spans(i), turned.pop(i)):
                 nc.vector.tensor_tensor(
                     out=grouped[:, 512 * groups.start : 512 * groups.stop].rearrange("p (q u e) -> p q u e", u=2, e=2),
@@ -202,11 +225,11 @@ def tile_reverb_prewhiten_replicas_s14_kernel(
                     in1=tp[:].bitcast(BF16).rearrange("p u (q e) -> p q u e", e=2),
                     op=ALU.mult,
                 )
+                give(("turned", i, groups.start))
             groupeds[i] = grouped
 
         def quant_past(i):
-            pc = work.tile([P, GROUPS * P], U32, align_bytes=64)
-            ps = work.tile([P, GROUPS * P], U8, align_bytes=64)
+            pc, ps = turn(ring_pc), turn(ring_ps)
             for groups in spans(i):
                 words = slice(P * groups.start, P * groups.stop)
                 nc.vector.quantize_mx(
@@ -215,11 +238,13 @@ def tile_reverb_prewhiten_replicas_s14_kernel(
                     in_=groupeds[i][:, 4 * words.start : 4 * words.stop],
                 )
             codes_p[i] = (pc, ps)
+            if i == 1:
+                give(("grouped", i))
 
         def predict(i):
             b = i // UNITS
             pc, ps = codes_p.pop(i)
-            pred = psum4.tile([P, NOW], F32, tag="mx")
+            pred = take(free_mx, ("pred", i))
             for g in range(GROUPS):
                 nc.tensor.matmul_mx(
                     out=pred[:],
@@ -234,13 +259,14 @@ def tile_reverb_prewhiten_replicas_s14_kernel(
 
         def empty_pred(i):
             if not vector_subtracts(i):
-                d = work.tile([P, 4, P], F32, align_bytes=64)
+                d = turn(ring_d).rearrange("r (t p) -> r t p", t=4)
                 nc.scalar.copy(out=d[:], in_=preds.pop(i)[:].rearrange("r (p t) -> r t p", t=4))
                 ds[i] = d
+                give(("pred", i))
 
         def subtract(i):
             if vector_subtracts(i):
-                d = work.tile([P, 4, P], F32, align_bytes=64)
+                d = turn(ring_d).rearrange("r (t p) -> r t p", t=4)
                 nc.vector.tensor_tensor(
                     out=d[:].rearrange("r (h e) p -> r h p e", h=2),
                     in0=preds.pop(i)[:].rearrange("r (p h e) -> r h p e", h=2, e=2),
@@ -248,6 +274,7 @@ def tile_reverb_prewhiten_replicas_s14_kernel(
                     op=ALU.subtract,
                 )
                 ds[i] = d
+                give(("pred", i))
 
         def take_now(i, slots):
             now_u = nows[i // UNITS][:, i % UNITS, :]
@@ -259,8 +286,7 @@ def tile_reverb_prewhiten_replicas_s14_kernel(
 
         def turn_now(i):
             if not lent(i):
-                dt = psum2.tile([P, 4, P], F32, tag="dt")
-                dts[i] = dt
+                dts[i] = take(free_dt, ("dt", i)).rearrange("p (t r) -> p t r", t=4)
             if not vector_subtracts(i):
                 take_now(i, range(1 if lent(i) else 0, 2))
 
@@ -276,15 +302,14 @@ def tile_reverb_prewhiten_replicas_s14_kernel(
 
         def lend(i):
             if lent(i):
-                dt = psum2.tile([P, 4, P], F32, tag="dt")
-                dts[i] = dt
+                dts[i] = take(free_dt, ("dt", i)).rearrange("p (t r) -> p t r", t=4)
                 take_now(i, range(1))
 
         def apply_taper(i):
             if i + ADD_LAG - 2 < STEPS:
-                e16 = work.tile([P, NOW], BF16, align_bytes=64)
+                e16 = turn(ring_e)
             else:
-                grouped = work.tile([P, 2 * WIDEST], BF16, align_bytes=64, bufs=GROUPEDS)
+                grouped = take(free_grouped, ("grouped", i + ADD_LAG - 2))
                 groupeds[i + ADD_LAG - 2] = grouped
                 e16 = grouped[:, :NOW]
             nc.vector.tensor_tensor(
@@ -293,11 +318,11 @@ def tile_reverb_prewhiten_replicas_s14_kernel(
                 in1=dts.pop(i)[:].rearrange("p t (a r) -> p a r t", r=REP),
                 op=ALU.mult,
             )
+            give(("dt", i))
             e16s[i] = e16
 
         def quant_e(i):
-            ec = work.tile([P, P], U32, align_bytes=64)
-            es = work.tile([P, P], U8, align_bytes=64)
+            ec, es = turn(ring_ec), turn(ring_es)
             nc.vector.quantize_mx(out=ec[:].bitcast(FP8X4), scales=es[:], in_=e16s.pop(i)[:])
             codes_e[i] = (ec, es)
 
@@ -309,12 +334,8 @@ def tile_reverb_prewhiten_replicas_s14_kernel(
         def correlate(i):
             b = i // UNITS
             ec, es = codes_e.pop(i)
-            if i >= STEPS - 4 and i % 2 == 0:
-                y_0 = psum2.tile([P, DOPPLER], F32, tag="turn")
-                y_1 = psum2.tile([P, DOPPLER], F32, tag="turn")
-            else:
-                y_0 = psum4.tile([P, DOPPLER], F32, tag="mx")
-                y_1 = psum4.tile([P, DOPPLER], F32, tag="mx")
+            free = free_turn if i >= STEPS - 4 and i % 2 == 0 else free_mx
+            y_0, y_1 = take(free, ("y", i, 0)), take(free, ("y", i, 1))
             if i == STEPS - 1:
                 parts = [(y, slice(256 * h, 256 * (h + 1)), DOPPLER * h + 256 * k) for k, y in enumerate((y_0, y_1)) for h in range(2)]
             else:
@@ -350,6 +371,7 @@ def tile_reverb_prewhiten_replicas_s14_kernel(
             home = squares(range(DOPPLER * i, DOPPLER * (i + 1)))
             for h in range(1 if i == STEPS - 2 else 2):
                 nc.scalar.activation(out=home[:, h, :], in_=ys[i][h][:], func=ACT.Square)
+                give(("y", i, h))
 
         def square_on_vector(i):
             held = keep.tile([P, DOPPLER], F32, align_bytes=64)
@@ -365,7 +387,7 @@ def tile_reverb_prewhiten_replicas_s14_kernel(
 
         def add_on_vector(i):
             sq = squares(piece(i))
-            total = work.tile([P, DOPPLER], F32, align_bytes=64, bufs=3)
+            total = turn(ring_total)
             if i == STEPS - 1:
                 for k in range(2):
                     nc.vector.tensor_tensor(
@@ -387,18 +409,22 @@ def tile_reverb_prewhiten_replicas_s14_kernel(
 
         def root(i):
             if i in sums:
-                env = outs.tile([P, WIDEST], F32, align_bytes=64, bufs=5)
+                env = turn(ring_env)
                 power = sums.pop(i)
                 for cols in pieces(i, power.shape[1]):
                     nc.scalar.activation(out=env[:, cols], in_=power[:, cols], func=ACT.Sqrt)
                     queue = nc.scalar if i == STEPS - 1 and cols.stop == DOPPLER else nc.sync
                     store(queue, piece(i).start + cols.start, env[:, cols])
+                give(("grouped", i + ADD_LAG))
 
         def helps(i):
             if i in groupeds:
                 home = groupeds.pop(i)[:, :PAST]
                 for j in [j for j in range(STEPS) if for_gpsimd(j) and cast[j] == 0][:1]:
                     widen(nc.gpsimd.tensor_copy, j, PAST, home)
+                    if ("grouped", i) in homes:
+                        homes[("raw", j)] = homes.pop(("grouped", i))
+                give(("grouped", i))
 
         def casts(s):
             widen_upto(s + 8)

from contextlib import ExitStack

import concourse.mybir as mybir
from concourse.masks import make_identity

BEAMS, PINGS, PAST, NOW, DOPPLER = 8, 512, 1024, 512, 512
FLOPS = 2 * BEAMS * PINGS * (PAST * NOW + NOW * 2 * DOPPLER)

P = 128
UNITS = PINGS // P
STEPS = BEAMS * UNITS
GROUPS = PAST // 512
ADD_LAG = 5
HELD = 4
TAIL = 2
SET = 5
CUTS = (0, 576, 1152, 1984, 2560)
LAST_SET = 20
GPSIMD_SUMS = 27
RING = 2 * SET
WIDEST = 832
EARLY = 3
LATE = 23
BEFORE_COPY = (9, 14, 18)
RAWS = 13
GROUPEDS = 9
REP = 8

F32 = mybir.dt.float32
BF16 = mybir.dt.bfloat16
U32 = mybir.dt.uint32
I32 = mybir.dt.int32
U8 = mybir.dt.uint8
FP8 = mybir.dt.float8_e4m3fn
FP8X4 = mybir.dt.float8_e4m3fn_x4
FP4X4 = mybir.dt.float4_e2m1fn_x4
ALU = mybir.AluOpType
ACT = mybir.ActivationFunctionType


def tile_reverb_prewhiten_replicas_s14_kernel(
    tc, past_bytes, past_scale, now, taper, coef_words, coef_scales, bank_words, bank_scales, out
):
    nc = tc.nc
    with ExitStack() as ctx:
        keep = ctx.enter_context(tc.tile_pool(name="keep", bufs=1))
        inp = ctx.enter_context(tc.tile_pool(name="inp", bufs=BEAMS))
        psum = ctx.enter_context(tc.psum_pool(name="psum", bufs=1))
        ctx.enter_context(tc.manual_schedule())

        coef_s = [keep.tile([P, GROUPS * NOW], U8, align_bytes=64, name="coef_s%d" % b) for b in range(HELD)] * 2
        bank_s = [keep.tile([P, 2 * DOPPLER], U8, align_bytes=64, name="bank_s%d" % b) for b in range(HELD)] * 2
        scale_sb = keep.tile([P, GROUPS, 4], F32, align_bytes=64)
        scale_x = keep.tile([P, GROUPS, P, 4], F32, align_bytes=64)
        taper_rows = keep.tile([P, NOW], BF16, align_bytes=64)
        taper_x = keep.tile([P, BEAMS, REP, 4], BF16, align_bytes=64)
        ident = keep.tile([P, P], F32, align_bytes=64)
        sq_ring = keep.tile([P, 2, RING * DOPPLER], F32, align_bytes=64)
        minus16 = keep.tile([P, P], BF16, align_bytes=64)

        def ring(pool, name, count, width, dtype):
            if pool is psum:
                return [pool.tile([P, width], dtype, name="%s%d" % (name, k))[:] for k in range(count)]
            return [pool.tile([P, width], dtype, align_bytes=64, name="%s%d" % (name, k))[:] for k in range(count)]

        free_turn, free_dt, free_mx = (ring(psum, n, c, 512, F32) for n, c in (("turn", 2), ("dt", 2), ("mx", 4)))
        free_raw = ring(keep, "raw", RAWS, PAST, BF16)
        free_grouped = ring(keep, "grouped", GROUPEDS, 2 * WIDEST, BF16)
        ring_pc, ring_ps = ring(keep, "pc", 4, GROUPS * P, U32), ring(keep, "ps", 4, GROUPS * P, U8)
        ring_ec, ring_es = ring(keep, "ec", 4, P, U32), ring(keep, "es", 4, P, U8)
        ring_d, ring_e = ring(keep, "d", 4, NOW, F32), ring(keep, "e", 4, NOW, BF16)
        ring_env, ring_total = ring(keep, "env", 5, WIDEST, F32), ring(keep, "total", 3, DOPPLER, F32)
        homes = {}

        def turn(tiles):
            tiles.append(tiles.pop(0))
            return tiles[-1]

        def take(free, key):
            homes[key] = (free, free.pop(0))
            return homes[key][1]

        def give(key):
            if key in homes:
                free, tile = homes.pop(key)
                free.append(tile)

        pasts, nows, coefs, banks = {}, {}, {}, {}
        whole = [(slice(0, UNITS), slice(0, PAST))]

        def load_past(b, pieces):
            if b not in pasts:
                past_u8 = inp.tile([P, UNITS, PAST], U8, align_bytes=64)
                pasts[b] = past_u8
            src = past_bytes[b].rearrange("(r j) k -> r j k", j=UNITS)
            for units, cols in pieces:
                nc.sync.dma_start(out=pasts[b][:, units, cols], in_=src[:, units, cols])

        def load_now(b):
            now_sb = inp.tile([P, UNITS, NOW], BF16, align_bytes=64, bufs=HELD)
            nc.sync.dma_start(out=now_sb[:], in_=now[b].rearrange("(r j) n -> r j n", j=UNITS))
            nows[b] = now_sb

        def load_coef(b):
            coef = inp.tile([P, GROUPS, 2 * NOW], U8, align_bytes=64, bufs=HELD)
            groups = slice(GROUPS * b, GROUPS * (b + 1))
            nc.sync.dma_start(out=coef[:].bitcast(I32), in_=coef_words[groups].rearrange("g p n -> p g n").bitcast(I32))
            coefs[b] = coef

        def load_coef_scales(b):
            groups = slice(GROUPS * b, GROUPS * (b + 1))
            for r in range(4):
                nc.sync.dma_start(
                    out=coef_s[b][r:P:32, :].rearrange("q (g n) -> q g n", g=GROUPS).bitcast(I32),
                    in_=coef_scales[groups, r:16:4, :].rearrange("g q n -> q g n").bitcast(I32),
                )

        def load_bank(b):
            bank = inp.tile([P, 4 * DOPPLER], U8, align_bytes=64, bufs=HELD)
            nc.sync.dma_start(out=bank[:].bitcast(I32), in_=bank_words[b].bitcast(I32))
            for r in range(4):
                nc.sync.dma_start(out=bank_s[b][r:P:32, :].bitcast(I32), in_=bank_scales[b, r:16:4, :].bitcast(I32))
            banks[b] = bank

        def load_beam(b):
            load_coef_scales(b)
            load_coef(b)
            load_now(b)
            if b + HELD < BEAMS:
                load_past(b + HELD, whole)
            load_bank(b)

        make_identity(nc, ident[:])
        nc.vector.memset(taper_rows[:].bitcast(F32), 0.0)
        for b in range(HELD):
            nc.vector.memset(coef_s[b][:].bitcast(I32), 0)
            nc.vector.memset(bank_s[b][:].bitcast(I32), 0)
        nc.scalar.activation(out=minus16[:], in_=ident[:], func=ACT.Sqrt)
        nc.vector.tensor_scalar(out=minus16[:], in0=minus16[:], scalar1=-1.0, scalar2=None, op0=ALU.mult)

        load_past(0, [(slice(0, 1), slice(0, 512))])
        nc.sync.dma_start(out=scale_sb[:], in_=past_scale.rearrange("a b (g p t) -> p (a b g) t", p=P, t=4))
        load_past(0, [(slice(0, 1), slice(512, PAST)), (slice(1, 2), slice(0, PAST)), (slice(2, UNITS), slice(0, PAST))])
        load_past(1, whole)
        nc.sync.dma_start(out=taper_rows[0:BEAMS, :], in_=taper)
        load_coef(0)
        load_coef_scales(0)
        load_past(2, whole)
        load_now(0)
        load_past(3, whole)
        load_bank(0)
        load_past(HELD, whole)
        for b in range(1, HELD):
            load_beam(b)

        for g in range(GROUPS):
            nc.vector.tensor_copy(out=scale_x[:, g], in_=scale_sb[:, g : g + 1, :].to_broadcast([P, P, 4]))

        def turn_taper():
            tp = take(free_dt, "taper")[:, : 2 * P].rearrange("p (u r) -> p u r", u=2)
            words = taper_rows[:].bitcast(F32)
            for u in range(2):
                nc.tensor.transpose(tp[:, u, :], words[:, u::2], ident[:])
            nc.scalar.activation(
                out=taper_x[:, :, 0, :].rearrange("p b (u e) -> p b u e", u=2),
                in_=tp[:].bitcast(BF16)[:, :, : 2 * BEAMS].rearrange("p u (b e) -> p b u e", e=2),
                func=ACT.Copy,
                scale=-1.0,
            )
            give("taper")

        def spread_taper():
            words = taper_x[:].bitcast(F32)
            nc.scalar.copy(out=words[:, :, 1:, :], in_=words[:, :, 0:1, :].to_broadcast([P, BEAMS, REP - 1, 2]))

        cast = [0] * STEPS
        raws, turned, groupeds, codes_p, preds, ds, dts, e16s, codes_e, ys, sums = ({} for k in range(11))

        def vector_subtracts(i):
            return (i % SET == 2 and i < LAST_SET + SET) or i >= STEPS - TAIL

        def for_gpsimd(i):
            return i % UNITS == UNITS - 1 or (i >= LATE and i % 2 == 1)

        def spans(i):
            return [range(g, g + 1) for g in range(GROUPS)] if i == 0 else [range(GROUPS)]

        def widen(copy, i, count, home=None):
            if i not in raws:
                if home is None:
                    home = take(free_raw, ("raw", i))
                raws[i] = home
            cols = slice(cast[i], min(cast[i] + count, PAST))
            copy(out=raws[i][:, cols], in_=pasts[i // UNITS][:, i % UNITS, cols].bitcast(FP8))
            cast[i] = cols.stop

        def widen_upto(units):
            for i in range(min(units, STEPS)):
                while cast[i] < PAST and not for_gpsimd(i):
                    widen(nc.scalar.copy, i, 512 if i == 0 else PAST)

        def turn_past(i):
            words = raws.pop(i).bitcast(F32)
            turned[i] = []
            for groups in spans(i):
                bank = take(free_mx if i == 3 or groups.start > 0 else free_turn, ("turned", i, groups.start))
                tp = bank[:, : 2 * len(groups) * P].rearrange("p (u r) -> p u r", u=2)
                for n, g in enumerate(groups):
                    for u in range(2):
                        nc.tensor.transpose(
                            tp[:, u, P * n : P * (n + 1)], words[:, 256 * g + u : 256 * (g + 1) : 2], ident[:]
                        )
                turned[i].append(tp)
            give(("raw", i))

        def scale_past(i):
            if i < ADD_LAG and i != 1:
                grouped = keep.tile([P, PAST], BF16, align_bytes=64, name="early%d" % i)[:]
            else:
                grouped = take(free_grouped, ("grouped", i))
            for groups, tp in zip(spans(i), turned.pop(i)):
                nc.vector.tensor_tensor(
                    out=grouped[:, 512 * groups.start : 512 * groups.stop].rearrange("p (q u e) -> p q u e", u=2, e=2),
                    in0=scale_x[:, groups.start : groups.stop].rearrange("p g r (u e) -> p (g r) u e", u=2),
                    in1=tp[:].bitcast(BF16).rearrange("p u (q e) -> p q u e", e=2),
                    op=ALU.mult,
                )
                give(("turned", i, groups.start))
            groupeds[i] = grouped

        def quant_past(i):
            pc, ps = turn(ring_pc), turn(ring_ps)
            for groups in spans(i):
                words = slice(P * groups.start, P * groups.stop)
                nc.vector.quantize_mx(
                    out=pc[:, words].bitcast(FP8X4),
                    scales=ps[:, words],
                    in_=groupeds[i][:, 4 * words.start : 4 * words.stop],
                )
            codes_p[i] = (pc, ps)
            if i == 1:
                give(("grouped", i))

        def predict(i):
            b = i // UNITS
            pc, ps = codes_p.pop(i)
            pred = take(free_mx, ("pred", i))
            for g in range(GROUPS):
                nc.tensor.matmul_mx(
                    out=pred[:],
                    lhsT=pc[:, P * g : P * (g + 1)].bitcast(FP8X4),
                    lhsT_scale=ps[:, P * g : P * (g + 1)],
                    rhs=coefs[b][:, g, :].bitcast(FP4X4),
                    rhs_scale=coef_s[b][:, NOW * g : NOW * (g + 1)],
                    start=(g == 0),
                    stop=(g == GROUPS - 1),
                )
            preds[i] = pred

        def empty_pred(i):
            if not vector_subtracts(i):
                d = turn(ring_d).rearrange("r (t p) -> r t p", t=4)
                nc.scalar.copy(out=d[:], in_=preds.pop(i)[:].rearrange("r (p t) -> r t p", t=4))
                ds[i] = d
                give(("pred", i))

        def subtract(i):
            if vector_subtracts(i):
                d = turn(ring_d).rearrange("r (t p) -> r t p", t=4)
                nc.vector.tensor_tensor(
                    out=d[:].rearrange("r (h e) p -> r h p e", h=2),
                    in0=preds.pop(i)[:].rearrange("r (p h e) -> r h p e", h=2, e=2),
                    in1=nows[i // UNITS][:, i % UNITS, :].rearrange("r (p h e) -> r h p e", h=2, e=2),
                    op=ALU.subtract,
                )
                ds[i] = d
                give(("pred", i))

        def take_now(i, slots):
            now_u = nows[i // UNITS][:, i % UNITS, :]
            for t in slots:
                nc.tensor.matmul(dts[i][:, t, :], lhsT=now_u[:, t::4], rhs=minus16[:], start=(t == 0), stop=(t == 3))

        def lent(i):
            return 0 < i < STEPS and vector_subtracts(i - 1) and not vector_subtracts(i)

        def turn_now(i):
            if not lent(i):
                dts[i] = take(free_dt, ("dt", i)).rearrange("p (t r) -> p t r", t=4)
            if not vector_subtracts(i):
                take_now(i, range(1 if lent(i) else 0, 2))

        def turn_d(i):
            d = ds.pop(i)
            alone = vector_subtracts(i)
            for t in range(4):
                nc.tensor.matmul(
                    dts[i][:, t, :], lhsT=d[:, t, :], rhs=ident[:], is_transpose=True, start=alone, stop=alone
                )
            if not alone:
                take_now(i, range(2, 4))

        def lend(i):
            if lent(i):
                dts[i] = take(free_dt, ("dt", i)).rearrange("p (t r) -> p t r", t=4)
                take_now(i, range(1))

        def apply_taper(i):
            if i + ADD_LAG - 2 < STEPS:
                e16 = turn(ring_e)
            else:
                grouped = take(free_grouped, ("grouped", i + ADD_LAG - 2))
                groupeds[i + ADD_LAG - 2] = grouped
                e16 = grouped[:, :NOW]
            nc.vector.tensor_tensor(
                out=e16[:].rearrange("p (a r t) -> p a r t", r=REP, t=4),
                in0=taper_x[:, i // UNITS].unsqueeze(1).to_broadcast([P, P // REP, REP, 4]),
                in1=dts.pop(i)[:].rearrange("p t (a r) -> p a r t", r=REP),
                op=ALU.mult,
            )
            give(("dt", i))
            e16s[i] = e16

        def quant_e(i):
            ec, es = turn(ring_ec), turn(ring_es)
            nc.vector.quantize_mx(out=ec[:].bitcast(FP8X4), scales=es[:], in_=e16s.pop(i)[:])
            codes_e[i] = (ec, es)

        def pieces(i, width):
            if i == STEPS - 1:
                return (slice(0, DOPPLER // 2), slice(DOPPLER // 2, DOPPLER))
            return (slice(0, width),)

        def correlate(i):
            b = i // UNITS
            ec, es = codes_e.pop(i)
            free = free_turn if i >= STEPS - 4 and i % 2 == 0 else free_mx
            y_0, y_1 = take(free, ("y", i, 0)), take(free, ("y", i, 1))
            if i == STEPS - 1:
                parts = [(y, slice(256 * h, 256 * (h + 1)), DOPPLER * h + 256 * k) for k, y in enumerate((y_0, y_1)) for h in range(2)]
            else:
                parts = [(y, slice(0, DOPPLER), DOPPLER * h) for h, y in enumerate((y_0, y_1))]
            for y, cols, first in parts:
                width = cols.stop - cols.start
                nc.tensor.matmul_mx(
                    out=y[:, cols],
                    lhsT=ec[:].bitcast(FP8X4),
                    lhsT_scale=es[:],
                    rhs=banks[b][:, 2 * first : 2 * (first + width)].bitcast(FP4X4),
                    rhs_scale=bank_s[b][:, first : first + width],
                    start=True,
                    stop=True,
                )
            ys[i] = (y_0, y_1)

        def piece(i):
            if i >= GPSIMD_SUMS:
                return range(DOPPLER * i, DOPPLER * (i + 1))
            first = DOPPLER * SET * min(i // SET, LAST_SET // SET)
            if i < LAST_SET:
                return range(first + CUTS[max(i % SET - 1, 0)], first + CUTS[i % SET])
            count = GPSIMD_SUMS - LAST_SET
            ends = [DOPPLER * count * k // (count - 1) // 16 * 16 for k in range(count)]
            return range(first + ends[max(i - LAST_SET - 1, 0)], first + ends[i - LAST_SET])

        def squares(cols):
            first = cols.start % (RING * DOPPLER)
            return sq_ring[:, :, first : first + len(cols)]

        def square(i):
            home = squares(range(DOPPLER * i, DOPPLER * (i + 1)))
            for h in range(1 if i == STEPS - 2 else 2):
                nc.scalar.activation(out=home[:, h, :], in_=ys[i][h][:], func=ACT.Square)
                give(("y", i, h))

        def square_on_vector(i):
            held = keep.tile([P, DOPPLER], F32, align_bytes=64)
            nc.vector.tensor_copy(out=held[:], in_=ys[i][1][:])
            nc.vector.tensor_tensor(out=squares(piece(i))[:, 1, :], in0=ys[i][1][:], in1=held[:], op=ALU.mult)

        def add(i):
            if piece(i):
                sq = squares(piece(i))
                power = groupeds.pop(i + ADD_LAG)[:].bitcast(F32)[:, : sq.shape[2]]
                nc.gpsimd.tensor_tensor(out=power, in0=sq[:, 0, :], in1=sq[:, 1, :], op=ALU.add)
                sums[i] = power

        def add_on_vector(i):
            sq = squares(piece(i))
            total = turn(ring_total)
            if i == STEPS - 1:
                for k in range(2):
                    nc.vector.tensor_tensor(
                        out=total[:, 256 * k : 256 * (k + 1)], in0=sq[:, k, :256], in1=sq[:, k, 256:], op=ALU.add
                    )
            else:
                nc.vector.tensor_tensor(out=total[:], in0=sq[:, 0, :], in1=sq[:, 1, :], op=ALU.add)
            sums[i] = total[:]

        def store(queue, first, env):
            row = UNITS * DOPPLER
            last = first + env.shape[1]
            for b in range(first // row, (last - 1) // row + 1):
                lo, hi = max(first, row * b), min(last, row * (b + 1))
                queue.dma_start(
                    out=out[b].rearrange("(r j) d -> r (j d)", j=UNITS)[:, lo - row * b : hi - row * b],
                    in_=env[:, lo - first : hi - first],
                )

        def root(i):
            if i in sums:
                env = turn(ring_env)
                power = sums.pop(i)
                for cols in pieces(i, power.shape[1]):
                    nc.scalar.activation(out=env[:, cols], in_=power[:, cols], func=ACT.Sqrt)
                    queue = nc.scalar if i == STEPS - 1 and cols.stop == DOPPLER else nc.sync
                    store(queue, piece(i).start + cols.start, env[:, cols])
                give(("grouped", i + ADD_LAG))

        def helps(i):
            if i in groupeds:
                home = groupeds.pop(i)[:, :PAST]
                for j in [j for j in range(STEPS) if for_gpsimd(j) and cast[j] == 0][:1]:
                    widen(nc.gpsimd.tensor_copy, j, PAST, home)
                    if ("grouped", i) in homes:
                        homes[("raw", j)] = homes.pop(("grouped", i))
                give(("grouped", i))

        def casts(s):
            widen_upto(s + 8)
            if s < EARLY or vector_subtracts(s + 3) or (s > STEPS // 2 and not piece(s - 2)):
                for j in [j for j in range(STEPS) if cast[j] < PAST and not for_gpsimd(j)][:1]:
                    widen_upto(j + 1)

        def run(*plan):
            for stage, i in plan:
                if 0 <= i < STEPS:
                    stage(i)

        widen_upto(3)
        widen(nc.gpsimd.tensor_copy, 3, PAST)
        run((turn_past, 0), (turn_past, 1))
        widen_upto(6)
        turn_taper()
        widen_upto(7)
        spread_taper()
        run((scale_past, 0), (turn_past, 2), (quant_past, 0), (helps, 0), (scale_past, 1), (predict, 0))
        widen_upto(BEFORE_COPY[0])
        run((turn_past, 3), (scale_past, 2), (empty_pred, 0))
        widen_upto(BEFORE_COPY[1])
        run((turn_past, 4), (turn_now, 0), (turn_d, 0))
        run((quant_past, 1), (quant_past, 2), (helps, 2), (predict, 1), (predict, 2), (scale_past, 3), (empty_pred, 1))
        widen_upto(BEFORE_COPY[2])
        run((empty_pred, 2), (turn_now, 1), (turn_past, 5), (turn_d, 1))
        for s in range(STEPS - 3):
            run((apply_taper, s), (lend, s + 2), (quant_past, s + 3), (quant_e, s), (add, s - 2), (helps, s + 3), (scale_past, s + 4))
            run((subtract, s + 2), (correlate, s), (predict, s + 3), (square, s), (empty_pred, s + 3), (root, s - 2))
            casts(s)
            run((turn_now, s + 2), (turn_past, s + 6), (turn_d, s + 2))
            if s >= UNITS and s % UNITS == 0 and s // UNITS + HELD - 1 < BEAMS:
                load_beam(s // UNITS + HELD - 1)
        a, b, c = range(STEPS - 3, STEPS)
        run((apply_taper, a), (quant_e, a), (add, a - 2), (subtract, c), (correlate, a), (turn_now, c), (turn_d, c))
        run((square, a), (root, a - 2), (apply_taper, b), (quant_e, b), (correlate, b), (square, b))
        run((apply_taper, c), (add_on_vector, a - 1), (quant_e, c), (correlate, c), (root, a - 1))
        run((add, a), (square_on_vector, b), (square, c), (root, a), (add_on_vector, b), (root, b))
        run((add_on_vector, c), (root, c))
